import numpy as np
import ml_dtypes


def mxq(x, axis, fmt="e4m3"):
    dtype, down = {"e4m3": (ml_dtypes.float8_e4m3fn, 7), "e5m2": (ml_dtypes.float8_e5m2, 14)}[fmt]
    v = np.moveaxis(np.asarray(x, np.float32).astype(ml_dtypes.bfloat16).astype(np.float64), axis, -1)
    blocks = v.reshape(v.shape[:-1] + (-1, 32))
    amax = np.abs(blocks).max(-1, keepdims=True)
    byte = np.maximum(np.where(amax > 0, np.frexp(amax)[1] - 1 + 127, 0) - down, 1)
    scale = np.exp2(byte - 127.0)
    codes = (blocks / scale).astype(np.float32).astype(dtype).astype(np.float64)
    return np.moveaxis((codes * scale).reshape(v.shape), -1, axis)


WIDE = False


def mx_kscale(k):
    if not WIDE:
        return np.ones(k)
    levels = np.array([10, -10, 5, -5, 0])
    if k % 512:
        return np.exp2(np.random.permutation(np.resize(levels, k // 32))).repeat(32)
    a = np.empty((k // 512, 16))
    for p in range(k // 512):
        a[p, :8] = np.random.permutation(np.resize(levels, 8))
        for g in range(8):
            far = levels[np.abs(levels - a[p, g]) >= 10]
            a[p, g + 8] = far[np.random.randint(len(far))]
    return np.exp2(a.ravel()).repeat(32)


def f64(x):
    return np.asarray(x).astype(np.float64)


def striped(idx):
    return np.tile(np.asarray(idx).reshape(-1, 16).T, (8, 1)).astype(np.uint16)


def unstriped(offs):
    return offs[:16].T.reshape(-1).astype(np.int64)


E2M1 = np.array([0.0, 0.5, 1.0, 1.5, 2.0, 3.0, 4.0, 6.0, -0.0, -0.5, -1.0, -1.5, -2.0, -3.0, -4.0, -6.0])


def pack_weight(w, fmt):
    k, n = w.shape
    w = f64(np.asarray(w, np.float32).astype(ml_dtypes.bfloat16)).reshape(k // 32, 32, n)
    amax = np.abs(w).max(1)
    if fmt == "e4m3":
        byte = np.frexp(amax)[1] - 1 + 127 - 7
    else:
        mant, ex = np.frexp(amax / 6.0)
        byte = np.where(mant > 0.5, ex, ex - 1) + 127
    byte = np.clip(np.where(amax > 0, byte, 1), 1, 254)
    scaled = (w * np.exp2(127.0 - byte)[:, None, :]).reshape(k, n).astype(np.float32)
    by_word = np.ascontiguousarray(scaled.reshape(k // 512, 128, 4, n).transpose(0, 1, 3, 2))
    if fmt == "e4m3":
        words = by_word.astype(ml_dtypes.float8_e4m3fn).view(np.uint8)
    else:
        c = by_word.astype(ml_dtypes.float4_e2m1fn).view(np.uint8) & 0xF
        words = (c[..., 0::2] | (c[..., 1::2] << 4)).reshape(k // 512, 128, 2 * n)
    return np.ascontiguousarray(words), np.ascontiguousarray(byte.astype(np.uint8).reshape(k // 512, 16, n))


def unpack_weight(words, scales, fmt):
    g, _, n = scales.shape
    words = np.ascontiguousarray(words).reshape(g, 128, n, -1)
    if fmt == "e4m3":
        vals = words.view(ml_dtypes.float8_e4m3fn).astype(np.float64)
    else:
        nib = np.empty((g, 128, n, 4), np.uint8)
        nib[..., 0::2] = words & 0xF
        nib[..., 1::2] = words >> 4
        vals = E2M1[nib]
    vals = vals * np.repeat(np.exp2(scales.astype(np.float64) - 127.0), 8, axis=1)[..., None]
    return vals.transpose(0, 1, 3, 2).reshape(g * 512, n)


D, T, I, Q, E, U, J = 512, 2048, 512, 128, 512, 1024, 512


def setup_inputs():
    n = np.random.standard_normal
    idx = np.random.permutation(T)[:I]
    idx2 = np.random.permutation(U)[:J]
    fd = mx_kscale(D)
    fi = mx_kscale(I)
    fj = mx_kscale(J)
    ti = np.ones(T)
    ti[idx] = fi
    tj = np.ones(U)
    tj[idx2] = fj
    keysp = pack_weight(n((D, T)) / fd[:, None], "e4m3")
    rkeyp = pack_weight(n((D, U)) / fd[:, None], "e2m1")
    return {
        "query": (n((D, Q)) * 0.4 / np.sqrt(D) * fd[:, None]).astype(np.float32),
        "keys_words": keysp[0],
        "keys_scales": keysp[1],
        "rkey_words": rkeyp[0],
        "rkey_scales": rkeyp[1],
        "size": (np.random.uniform(0.5, 2.0, (1, I)) * fi).astype(np.float32),
        "rsz": (np.random.uniform(0.5, 2.0, (1, J)) * fj).astype(np.float32),
        "vals": (n((E, T)) / ti).astype(np.float32),
        "rval": (n((E, U)) / tj).astype(np.float32),
        "offs": striped(idx),
        "offs2": striped(idx2),
    }


def reference(query, keys_words, keys_scales, rkey_words, rkey_scales, size, rsz, vals, rval, offs, offs2):
    idx = unstriped(offs)
    idx2 = unstriped(offs2)
    keysu = unpack_weight(keys_words, keys_scales, "e4m3")
    rkeyu = unpack_weight(rkey_words, rkey_scales, "e2m1")
    queryq = mxq(f64(query), 0, "e4m3")
    keysidxg = keysu[:, idx]
    a = queryq.T @ keysidxg
    rkeyidx2g = rkeyu[:, idx2]
    b = queryq.T @ rkeyidx2g
    m = np.maximum(np.max(a, axis=1, keepdims=True), np.max(b, axis=1, keepdims=True))
    p = np.exp(a - m)
    r = np.exp(b - m)
    z = np.sum(p, axis=1, keepdims=True) + np.sum(r, axis=1, keepdims=True)
    w = p * f64(size) / z
    x = r * f64(rsz) / z
    wt = w.T
    xt = x.T
    vt = f64(vals)[:, idx].T
    ut = f64(rval)[:, idx2].T
    wtq = mxq(wt, 0, "e4m3")
    vtq = mxq(vt, 0, "e4m3")
    xtq = mxq(xt, 0, "e4m3")
    utq = mxq(ut, 0, "e4m3")
    o = wtq.T @ vtq + xtq.T @ utq
    return o

@@ -1,0 +1,172 @@
+from contextlib import ExitStack
+
+import concourse.mybir as mybir
+from concourse.masks import make_identity
+
+F32 = mybir.dt.float32
+BF16 = mybir.dt.bfloat16
+I32 = mybir.dt.int32
+U32 = mybir.dt.uint32
+U16 = mybir.dt.uint16
+U8 = mybir.dt.uint8
+FP8X4 = mybir.dt.float8_e4m3fn_x4
+FP4X4 = mybir.dt.float4_e2m1fn_x4
+ACT = mybir.ActivationFunctionType
+ALU = mybir.AluOpType
+AX = mybir.AxisListType
+
+P = 128
+D, T, I, Q, E, U, J = 512, 2048, 512, 128, 512, 1024, 512
+NB = E // P
+FLOPS = 2 * Q * D * (I + J) + 2 * Q * E * (I + J)
+ON_SCALAR = 2
+
+
+def tile_attend_two_caches_kernel(tc, query, keys_words, keys_scales, rkey_words, rkey_scales, size, rsz, vals, rval, offs, offs2, out):
+    nc = tc.nc
+    with ExitStack() as ctx:
+        sb = ctx.enter_context(tc.tile_pool(name="sb", bufs=1))
+        ps = ctx.enter_context(tc.psum_pool(name="ps", bufs=1))
+        turn = ctx.enter_context(tc.psum_pool(name="turn", bufs=3))
+
+        def sbuf(name, shape, dtype):
+            return sb.tile(shape, dtype, name=name, align_bytes=64)
+
+        lst = sbuf("lst", [P, I // 16], U16)
+        lst2 = sbuf("lst2", [P, J // 16], U16)
+        kw = sbuf("kw", [P, T], U32)
+        ks = sbuf("ks", [P, T], U8)
+        rw = sbuf("rw", [P, U], U16)
+        rs = sbuf("rs", [P, U], U8)
+        qraw = sbuf("qraw", [P, 4, Q], F32)
+        szc = sbuf("szc", [P, 4], F32)
+        rszc = sbuf("rszc", [P, 4], F32)
+        vpool = [sbuf("vpool%d" % k, [P, T], F32) for k in range(NB)]
+        upool = [sbuf("upool%d" % k, [P, U], F32) for k in range(NB)]
+        ident = sbuf("ident", [P, P], F32)
+        warm = sbuf("warm", [P, 8], F32)
+
+        nc.gpsimd.memset(rs[:].bitcast(I32), 0)
+        nc.gpsimd.memset(ks[:].bitcast(I32), 0)
+        make_identity(nc, ident[:])
+
+        def load_scales(plane, scales):
+            for g in range(4):
+                nc.sync.dma_start(out=plane[32 * g : 32 * g + 4, :].bitcast(I32), in_=scales[0, 4 * g : 4 * g + 4, :].bitcast(I32))
+
+        nc.sync.dma_start(lst2[:], offs2)
+        nc.sync.dma_start(out=rw[:].bitcast(I32), in_=rkey_words[0].bitcast(I32))
+        nc.sync.dma_start(lst[:], offs)
+        nc.sync.dma_start(out=qraw[:], in_=query.rearrange("(p j) w -> p j w", j=4))
+        load_scales(rs, rkey_scales)
+        nc.sync.dma_start(out=kw[:].bitcast(I32), in_=keys_words[0].rearrange("p n t -> p (n t)").bitcast(I32))
+        nc.sync.dma_start(out=upool[0][:], in_=rval[0:P, :])
+        load_scales(ks, keys_scales)
+        for k in range(1, NB):
+            nc.sync.dma_start(out=upool[k][:], in_=rval[k * P : (k + 1) * P, :])
+        nc.sync.dma_start(out=szc[:], in_=size[0].rearrange("(p t) -> p t", t=4))
+        nc.sync.dma_start(out=rszc[:], in_=rsz[0].rearrange("(p t) -> p t", t=4))
+        for k in range(NB):
+            nc.sync.dma_start(out=vpool[k][:], in_=vals[k * P : (k + 1) * P, :])
+
+        nc.vector.memset(warm[:], 0.0)
+        nc.scalar.activation(out=warm[:, 0:1], in_=warm[:, 4:5], func=ACT.Exp)
+
+        rwg = sbuf("rwg", [P, J], U16)
+        rsg = sbuf("rsg", [P, J], U8)
+        kwg = sbuf("kwg", [P, I], U32)
+        ksg = sbuf("ksg", [P, I], U8)
+        nc.vector.tensor_copy(rwg[:], rw[:].indirect(lst2[:]))
+        nc.vector.tensor_copy(rsg[:], rs[:].indirect(lst2[:]))
+        nc.vector.tensor_copy(kwg[:], kw[:].indirect(lst[:]))
+        qb = sbuf("qb", [P, Q, 4], BF16)
+        nc.scalar.copy(out=qb[:], in_=qraw[:].rearrange("p j w -> p w j"))
+        qc = sbuf("qc", [P, Q], U32)
+        qs = sbuf("qs", [P, Q], U8)
+        nc.vector.quantize_mx(out=qc[:].bitcast(FP8X4), scales=qs[:], in_=qb[:].rearrange("p w j -> p (w j)"))
+        nc.vector.tensor_copy(ksg[:], ks[:].indirect(lst[:]))
+
+        sc_b = ps.tile([P, J], F32, name="sc_b", tag="bank0")
+        sc_a = ps.tile([P, I], F32, name="sc_a", tag="bank1")
+        nc.tensor.matmul_mx(out=sc_b[:], lhsT=qc[:].bitcast(FP8X4), lhsT_scale=qs[:], rhs=rwg[:].bitcast(FP4X4), rhs_scale=rsg[:], start=True, stop=True)
+        nc.tensor.matmul_mx(out=sc_a[:], lhsT=qc[:].bitcast(FP8X4), lhsT_scale=qs[:], rhs=kwg[:].bitcast(FP8X4), rhs_scale=ksg[:], start=True, stop=True)
+
+        spread = []
+        for name, col, tag in (("szb", szc, "bank2"), ("rszb", rszc, "bank3")):
+            bank = ps.tile([P, 4, P], F32, name=name, tag=tag)
+            for t in range(4):
+                nc.tensor.transpose(bank[:, t, :], col[:, t : t + 1].to_broadcast([P, P]), ident[:])
+            spread.append(bank)
+
+        def turn_words(src, dst):
+            words = src.bitcast(F32)
+            bank = turn.tile([P, 2, P], F32, name="bank")
+            for u in range(2):
+                nc.tensor.transpose(bank[:, u, :], words[:, u : 2 * P : 2], ident[:])
+            nc.scalar.copy(out=dst.bitcast(F32), in_=bank[:].rearrange("p u r -> p r u"))
+
+        ut = sbuf("ut", [P, E, 4], BF16)
+        ug = [sbuf("ug%d" % k, [P, J], BF16) for k in range(NB)]
+
+        def gather_rval(k):
+            if k < ON_SCALAR:
+                ub = sbuf("ub%d" % k, [P, U], BF16)
+                nc.scalar.activation(out=ub[:], in_=upool[k][:], func=ACT.Copy)
+                nc.scalar.activation(out=ug[k][:], in_=ub[:].indirect(lst2[:]), func=ACT.Copy)
+            else:
+                nc.vector.tensor_copy(ug[k][:], upool[k][:].indirect(lst2[:]))
+            turn_words(ug[k][:], ut[:, k * P : (k + 1) * P, :])
+
+        negb = sbuf("negb", [P, 1], F32)
+        negm = sbuf("negm", [P, 1], F32)
+        nega = sbuf("nega", [P, I], F32)
+        nc.vector.tensor_reduce(out=negb[:], in_=sc_b[:], axis=AX.X, op=ALU.max, negate=True)
+        nc.vector.tensor_scalar(out=nega[:], in0=sc_a[:], scalar1=-1.0, scalar2=negb[:], op0=ALU.mult, op1=ALU.min, accum_out=negm[:])
+        pa = sbuf("pa", [P, I], F32)
+        pb = sbuf("pb", [P, J], F32)
+        za = sbuf("za", [P, 1], F32)
+        zb = sbuf("zb", [P, 1], F32)
+        z = sbuf("z", [P, 1], F32)
+        rz = sbuf("rz", [P, 1], F32)
+        nc.scalar.activation(out=pb[:], in_=sc_b[:], func=ACT.Exp, bias=negm[:], accum_out=zb[:])
+        nc.scalar.activation(out=pa[:], in_=nega[:], func=ACT.Exp, bias=negm[:], scale=-1.0, accum_out=za[:])
+        nc.scalar.activation(out=z[:], in_=za[:], func=ACT.Identity, bias=zb[:])
+        for k in range(NB):
+            gather_rval(k)
+        nc.vector.reciprocal(out=rz[:], in_=z[:])
+        wb = sbuf("wb", [P, I], BF16)
+        xb = sbuf("xb", [P, J], BF16)
+        wxt = sbuf("wxt", [P, 2 * Q, 4], BF16)
+        for n, (dst, prob) in enumerate(((wb, pa), (xb, pb))):
+            nc.vector.scalar_tensor_tensor(
+                out=dst[:].rearrange("q (s t) -> q s t", t=4),
+                in0=prob[:].rearrange("q (s t) -> q s t", t=4),
+                scalar=rz[:],
+                in1=spread[n][:].rearrange("q t s -> q s t"),
+                op0=ALU.mult,
+                op1=ALU.mult,
+            )
+            turn_words(dst[:], wxt[:, n * Q : (n + 1) * Q, :])
+        uc = sbuf("uc", [P, E], U32)
+        us = sbuf("us", [P, E], U8)
+        nc.vector.quantize_mx(out=uc[:].bitcast(FP8X4), scales=us[:], in_=ut[:].rearrange("p e t -> p (e t)"))
+        wxc = sbuf("wxc", [P, 2 * Q], U32)
+        wxs = sbuf("wxs", [P, 2 * Q], U8)
+        nc.vector.quantize_mx(out=wxc[:].bitcast(FP8X4), scales=wxs[:], in_=wxt[:].rearrange("p e t -> p (e t)"))
+
+        acc = [ps.tile([P, P], F32, name="acc%d" % k, tag="bank%d" % k) for k in range(NB)]
+        for k in range(NB):
+            cols = slice(k * P, (k + 1) * P)
+            nc.tensor.matmul_mx(out=acc[k][:], lhsT=wxc[:, Q : 2 * Q].bitcast(FP8X4), lhsT_scale=wxs[:, Q : 2 * Q], rhs=uc[:, cols].bitcast(FP8X4), rhs_scale=us[:, cols], start=True, stop=False)
+        for k in range(NB):
+            vg = sbuf("vg%d" % k, [P, I], BF16)
+            vt = sbuf("vt%d" % k, [P, P, 4], BF16)
+            vc = sbuf("vc%d" % k, [P, P], U32)
+            vs = sbuf("vs%d" % k, [P, P], U8)
+            res = sbuf("res%d" % k, [P, P], F32)
+            nc.vector.tensor_copy(vg[:], vpool[k][:].indirect(lst[:]))
+            turn_words(vg[:], vt[:])
+            nc.vector.quantize_mx(out=vc[:].bitcast(FP8X4), scales=vs[:], in_=vt[:].rearrange("p e t -> p (e t)"))
+            nc.tensor.matmul_mx(out=acc[k][:], lhsT=wxc[:, 0:Q].bitcast(FP8X4), lhsT_scale=wxs[:, 0:Q], rhs=vc[:].bitcast(FP8X4), rhs_scale=vs[:], start=False, stop=True)
+            nc.scalar.copy(out=res[:], in_=acc[k][:])
+            nc.sync.dma_start(out=out[:, k * P : (k + 1) * P], in_=res[:])

@@ -18,8 +18,8 @@ AX = mybir.AxisListType
 P = 128
 D, T, I, Q, E, U, J = 512, 2048, 512, 128, 512, 1024, 512
 NB = E // P
+BIG = 3.0e38
 FLOPS = 2 * Q * D * (I + J) + 2 * Q * E * (I + J)
-ON_SCALAR = 2
 
 
 def tile_attend_two_caches_kernel(tc, query, keys_words, keys_scales, rkey_words, rkey_scales, size, rsz, vals, rval, offs, offs2, out):
@@ -27,10 +27,10 @@ def tile_attend_two_caches_kernel(tc, query, keys_words, keys_scales, rkey_words
     with ExitStack() as ctx:
         sb = ctx.enter_context(tc.tile_pool(name="sb", bufs=1))
         ps = ctx.enter_context(tc.psum_pool(name="ps", bufs=1))
-        turn = ctx.enter_context(tc.psum_pool(name="turn", bufs=3))
+        turn = ctx.enter_context(tc.psum_pool(name="turn", bufs=4))
 
-        def sbuf(name, shape, dtype):
-            return sb.tile(shape, dtype, name=name, align_bytes=64)
+        def sbuf(name, shape, dtype, after=None):
+            return sb.tile(shape, dtype, name=name, tag=after or name, align_bytes=64)
 
         lst = sbuf("lst", [P, I // 16], U16)
         lst2 = sbuf("lst2", [P, J // 16], U16)
@@ -50,20 +50,24 @@ def tile_attend_two_caches_kernel(tc, query, keys_words, keys_scales, rkey_words
         nc.gpsimd.memset(ks[:].bitcast(I32), 0)
         make_identity(nc, ident[:])
 
-        def load_scales(plane, scales):
+        def load_scales(plane, scales, row):
             for g in range(4):
-                nc.sync.dma_start(out=plane[32 * g : 32 * g + 4, :].bitcast(I32), in_=scales[0, 4 * g : 4 * g + 4, :].bitcast(I32))
+                nc.sync.dma_start(out=plane[32 * g + row : 32 * g + row + 4, :].bitcast(I32), in_=scales[0, 4 * g : 4 * g + 4, :].bitcast(I32))
+
+        def load_rval(k):
+            nc.sync.dma_start(out=upool[k][:], in_=rval[k * P : (k + 1) * P, :])
 
         nc.sync.dma_start(lst2[:], offs2)
         nc.sync.dma_start(out=rw[:].bitcast(I32), in_=rkey_words[0].bitcast(I32))
-        nc.sync.dma_start(lst[:], offs)
+        load_rval(2)
+        load_rval(3)
         nc.sync.dma_start(out=qraw[:], in_=query.rearrange("(p j) w -> p j w", j=4))
-        load_scales(rs, rkey_scales)
+        load_scales(rs, rkey_scales, 0)
         nc.sync.dma_start(out=kw[:].bitcast(I32), in_=keys_words[0].rearrange("p n t -> p (n t)").bitcast(I32))
-        nc.sync.dma_start(out=upool[0][:], in_=rval[0:P, :])
-        load_scales(ks, keys_scales)
-        for k in range(1, NB):
-            nc.sync.dma_start(out=upool[k][:], in_=rval[k * P : (k + 1) * P, :])
+        nc.sync.dma_start(lst[:], offs)
+        load_scales(ks, keys_scales, 4)
+        load_rval(0)
+        load_rval(1)
         nc.sync.dma_start(out=szc[:], in_=size[0].rearrange("(p t) -> p t", t=4))
         nc.sync.dma_start(out=rszc[:], in_=rsz[0].rearrange("(p t) -> p t", t=4))
         for k in range(NB):
@@ -72,24 +76,63 @@ def tile_attend_two_caches_kernel(tc, query, keys_words, keys_scales, rkey_words
         nc.vector.memset(warm[:], 0.0)
         nc.scalar.activation(out=warm[:, 0:1], in_=warm[:, 4:5], func=ACT.Exp)
 
+        def turn_words(sources, dst, bank=None):
+            n = len(sources)
+            if bank is None:
+                bank = turn.tile([P, n, 2, P], F32, name="bank")
+            for b, src in enumerate(sources):
+                words = src[:].bitcast(F32)
+                for u in range(2):
+                    nc.tensor.transpose(bank[:, b, u, :], words[:, u : 2 * P : 2], ident[:])
+            nc.scalar.copy(out=dst.bitcast(F32).rearrange("p (b r) u -> p b r u", b=n), in_=bank[:].rearrange("p b u r -> p b r u"))
+
+        def quantise(name, src, after=None):
+            cols = src.shape[1]
+            codes = sbuf(name + "c", [P, cols], U32, after)
+            plane = sbuf(name + "s", [P, cols], U8)
+            nc.vector.quantize_mx(out=codes[:].bitcast(FP8X4), scales=plane[:], in_=src.rearrange("p e t -> p (e t)"))
+            return codes, plane
+
+        def product(dst, left, lcol, right, rcol, width, start, stop):
+            lc, rc = slice(lcol, lcol + P), slice(rcol, rcol + width)
+            nc.tensor.matmul_mx(out=dst, lhsT=left[0][:, lc].bitcast(FP8X4), lhsT_scale=left[1][:, lc], rhs=right[0][:, rc].bitcast(FP8X4), rhs_scale=right[1][:, rc], start=start, stop=stop)
+
+        def cast_rval(k, after=None):
+            ub = sbuf("ub%d" % k, [P, U], BF16, after)
+            nc.scalar.activation(out=ub[:], in_=upool[k][:], func=ACT.Copy)
+            return ub
+
+        def gather_scalar(k, ub, after=None):
+            ug = sbuf("ug%d" % k, [P, J], BF16, after)
+            nc.scalar.activation(out=ug[:], in_=ub[:].indirect(lst2[:]), func=ACT.Copy)
+            return ug
+
+        def gather_vector(name, pool_tile, offsets, after=None):
+            picked = sbuf(name, [P, J], BF16, after)
+            nc.vector.tensor_copy(picked[:], pool_tile[:].indirect(offsets[:]))
+            return picked
+
         rwg = sbuf("rwg", [P, J], U16)
-        rsg = sbuf("rsg", [P, J], U8)
         kwg = sbuf("kwg", [P, I], U32)
         ksg = sbuf("ksg", [P, I], U8)
         nc.vector.tensor_copy(rwg[:], rw[:].indirect(lst2[:]))
+        ug2 = gather_vector("ug2", upool[2], lst2)
+        ug3 = gather_scalar(3, cast_rval(3))
+        rsg = sbuf("rsg", [P, J], U8)
         nc.vector.tensor_copy(rsg[:], rs[:].indirect(lst2[:]))
-        nc.vector.tensor_copy(kwg[:], kw[:].indirect(lst[:]))
         qb = sbuf("qb", [P, Q, 4], BF16)
-        nc.scalar.copy(out=qb[:], in_=qraw[:].rearrange("p j w -> p w j"))
-        qc = sbuf("qc", [P, Q], U32)
-        qs = sbuf("qs", [P, Q], U8)
-        nc.vector.quantize_mx(out=qc[:].bitcast(FP8X4), scales=qs[:], in_=qb[:].rearrange("p w j -> p (w j)"))
+        nc.vector.tensor_copy(out=qb[:], in_=qraw[:].rearrange("p j w -> p w j"))
+        qc, qs = quantise("q", qb[:])
+        mid = sbuf("mid", [P, 4 * P, 4], BF16)
+        late = sbuf("late", [P, 4 * P, 4], BF16)
+        turn_words([ug2, ug3], mid[:, 0 : 2 * P, :], ps.tile([P, 2, 2, P], F32, name="bank23", tag="bank0"))
+        nc.vector.tensor_copy(kwg[:], kw[:].indirect(lst[:]))
         nc.vector.tensor_copy(ksg[:], ks[:].indirect(lst[:]))
 
         sc_b = ps.tile([P, J], F32, name="sc_b", tag="bank0")
         sc_a = ps.tile([P, I], F32, name="sc_a", tag="bank1")
         nc.tensor.matmul_mx(out=sc_b[:], lhsT=qc[:].bitcast(FP8X4), lhsT_scale=qs[:], rhs=rwg[:].bitcast(FP4X4), rhs_scale=rsg[:], start=True, stop=True)
-        nc.tensor.matmul_mx(out=sc_a[:], lhsT=qc[:].bitcast(FP8X4), lhsT_scale=qs[:], rhs=kwg[:].bitcast(FP8X4), rhs_scale=ksg[:], start=True, stop=True)
+        nc.tensor.matmul_mx(out=sc_a[:], lhsT=qc[:].bitcast(FP8X4), lhsT_scale=qs[:], rhs=kwg[:].bitcast(FP8X4), rhs_scale=ksg[4:P, :], start=True, stop=True)
 
         spread = []
         for name, col, tag in (("szb", szc, "bank2"), ("rszb", rszc, "bank3")):
@@ -98,75 +141,59 @@ def tile_attend_two_caches_kernel(tc, query, keys_words, keys_scales, rkey_words
                 nc.tensor.transpose(bank[:, t, :], col[:, t : t + 1].to_broadcast([P, P]), ident[:])
             spread.append(bank)
 
-        def turn_words(src, dst):
-            words = src.bitcast(F32)
-            bank = turn.tile([P, 2, P], F32, name="bank")
-            for u in range(2):
-                nc.tensor.transpose(bank[:, u, :], words[:, u : 2 * P : 2], ident[:])
-            nc.scalar.copy(out=dst.bitcast(F32), in_=bank[:].rearrange("p u r -> p r u"))
+        ub0 = cast_rval(0, after="ug3")
+        ub1 = cast_rval(1)
 
-        ut = sbuf("ut", [P, E, 4], BF16)
-        ug = [sbuf("ug%d" % k, [P, J], BF16) for k in range(NB)]
-
-        def gather_rval(k):
-            if k < ON_SCALAR:
-                ub = sbuf("ub%d" % k, [P, U], BF16)
-                nc.scalar.activation(out=ub[:], in_=upool[k][:], func=ACT.Copy)
-                nc.scalar.activation(out=ug[k][:], in_=ub[:].indirect(lst2[:]), func=ACT.Copy)
-            else:
-                nc.vector.tensor_copy(ug[k][:], upool[k][:].indirect(lst2[:]))
-            turn_words(ug[k][:], ut[:, k * P : (k + 1) * P, :])
-
-        negb = sbuf("negb", [P, 1], F32)
+        start = sbuf("start", [P, 1], F32, after="kw")
         negm = sbuf("negm", [P, 1], F32)
-        nega = sbuf("nega", [P, I], F32)
-        nc.vector.tensor_reduce(out=negb[:], in_=sc_b[:], axis=AX.X, op=ALU.max, negate=True)
-        nc.vector.tensor_scalar(out=nega[:], in0=sc_a[:], scalar1=-1.0, scalar2=negb[:], op0=ALU.mult, op1=ALU.min, accum_out=negm[:])
-        pa = sbuf("pa", [P, I], F32)
-        pb = sbuf("pb", [P, J], F32)
-        za = sbuf("za", [P, 1], F32)
-        zb = sbuf("zb", [P, 1], F32)
+        neg = sbuf("neg", [P, I + J], F32)
+        nc.vector.tensor_scalar(out=neg[:, I : I + J], in0=sc_b[:], scalar1=-1.0, scalar2=BIG, op0=ALU.mult, op1=ALU.min, accum_out=start[:])
+        nc.vector.tensor_scalar(out=neg[:, 0:I], in0=sc_a[:], scalar1=-1.0, scalar2=start[:], op0=ALU.mult, op1=ALU.min, accum_out=negm[:])
+        prob = sbuf("prob", [P, I + J], F32, after="upool1")
         z = sbuf("z", [P, 1], F32)
-        rz = sbuf("rz", [P, 1], F32)
-        nc.scalar.activation(out=pb[:], in_=sc_b[:], func=ACT.Exp, bias=negm[:], accum_out=zb[:])
-        nc.scalar.activation(out=pa[:], in_=nega[:], func=ACT.Exp, bias=negm[:], scale=-1.0, accum_out=za[:])
-        nc.scalar.activation(out=z[:], in_=za[:], func=ACT.Identity, bias=zb[:])
-        for k in range(NB):
-            gather_rval(k)
+        nc.scalar.activation(out=prob[:], in_=neg[:], func=ACT.Exp, bias=negm[:], scale=-1.0, accum_out=z[:])
+
+        ug0 = gather_scalar(0, ub0, after="neg")
+        ug1 = gather_scalar(1, ub1, after="negm")
+
+        vg0 = gather_vector("vg0", vpool[0], lst)
+        rz = sbuf("rz", [P, 1], F32, after="vpool0")
         nc.vector.reciprocal(out=rz[:], in_=z[:])
-        wb = sbuf("wb", [P, I], BF16)
-        xb = sbuf("xb", [P, J], BF16)
-        wxt = sbuf("wxt", [P, 2 * Q, 4], BF16)
-        for n, (dst, prob) in enumerate(((wb, pa), (xb, pb))):
+        weights = []
+        for n in range(2):
+            weight = sbuf("weight%d" % n, [P, I], BF16)
             nc.vector.scalar_tensor_tensor(
-                out=dst[:].rearrange("q (s t) -> q s t", t=4),
-                in0=prob[:].rearrange("q (s t) -> q s t", t=4),
+                out=weight[:].rearrange("q (s t) -> q s t", t=4),
+                in0=prob[:, n * I : (n + 1) * I].rearrange("q (s t) -> q s t", t=4),
                 scalar=rz[:],
                 in1=spread[n][:].rearrange("q t s -> q s t"),
                 op0=ALU.mult,
                 op1=ALU.mult,
             )
-            turn_words(dst[:], wxt[:, n * Q : (n + 1) * Q, :])
-        uc = sbuf("uc", [P, E], U32)
-        us = sbuf("us", [P, E], U8)
-        nc.vector.quantize_mx(out=uc[:].bitcast(FP8X4), scales=us[:], in_=ut[:].rearrange("p e t -> p (e t)"))
-        wxc = sbuf("wxc", [P, 2 * Q], U32)
-        wxs = sbuf("wxs", [P, 2 * Q], U8)
-        nc.vector.quantize_mx(out=wxc[:].bitcast(FP8X4), scales=wxs[:], in_=wxt[:].rearrange("p e t -> p (e t)"))
+            weights.append(weight)
+        turn_words(weights, mid[:, 2 * P : 4 * P, :])
 
-        acc = [ps.tile([P, P], F32, name="acc%d" % k, tag="bank%d" % k) for k in range(NB)]
-        for k in range(NB):
-            cols = slice(k * P, (k + 1) * P)
-            nc.tensor.matmul_mx(out=acc[k][:], lhsT=wxc[:, Q : 2 * Q].bitcast(FP8X4), lhsT_scale=wxs[:, Q : 2 * Q], rhs=uc[:, cols].bitcast(FP8X4), rhs_scale=us[:, cols], start=True, stop=False)
-        for k in range(NB):
-            vg = sbuf("vg%d" % k, [P, I], BF16)
-            vt = sbuf("vt%d" % k, [P, P, 4], BF16)
-            vc = sbuf("vc%d" % k, [P, P], U32)
-            vs = sbuf("vs%d" % k, [P, P], U8)
-            res = sbuf("res%d" % k, [P, P], F32)
-            nc.vector.tensor_copy(vg[:], vpool[k][:].indirect(lst[:]))
-            turn_words(vg[:], vt[:])
-            nc.vector.quantize_mx(out=vc[:].bitcast(FP8X4), scales=vs[:], in_=vt[:].rearrange("p e t -> p (e t)"))
-            nc.tensor.matmul_mx(out=acc[k][:], lhsT=wxc[:, 0:Q].bitcast(FP8X4), lhsT_scale=wxs[:, 0:Q], rhs=vc[:].bitcast(FP8X4), rhs_scale=vs[:], start=False, stop=True)
-            nc.scalar.copy(out=res[:], in_=acc[k][:])
-            nc.sync.dma_start(out=out[:, k * P : (k + 1) * P], in_=res[:])
+        tail = [sbuf("tail%d" % k, [P, P, 4], BF16) for k in range(2)]
+        vg1 = gather_vector("vg1", vpool[1], lst)
+        turn_words([ug0, ug1], late[:, 0 : 2 * P, :], ps.tile([P, 2, 2, P], F32, name="bank01", tag="bank3"))
+        turn_words([vg0, vg1], late[:, 2 * P : 4 * P, :])
+        turn_words([gather_vector("vg2", vpool[2], lst)], tail[0][:])
+        mid_q = quantise("midq", mid[:], after="vpool2")
+        turn_words([gather_vector("vg3", vpool[3], lst)], tail[1][:])
+        late_q = quantise("lateq", late[:], after="vpool3")
+        tail_q = [quantise("tail0q", tail[0][:], after="late"), quantise("tail1q", tail[1][:])]
+
+        acc2 = ps.tile([P, P], F32, name="acc2", tag="bank1")
+        acc3 = ps.tile([P, P], F32, name="acc3", tag="bank2")
+        acc01 = ps.tile([P, 2 * P], F32, name="acc01", tag="bank0")
+        product(acc2[:], mid_q, 3 * P, mid_q, 0, P, True, False)
+        product(acc3[:], mid_q, 3 * P, mid_q, P, P, True, False)
+        product(acc01[:], mid_q, 3 * P, late_q, 0, 2 * P, True, False)
+        product(acc01[:], mid_q, 2 * P, late_q, 2 * P, 2 * P, False, True)
+        product(acc2[:], mid_q, 2 * P, tail_q[0], 0, P, False, True)
+        product(acc3[:], mid_q, 2 * P, tail_q[1], 0, P, False, True)
+        for name, acc, col, engine_copy in (("res01", acc01, 0, nc.scalar.copy), ("res2", acc2, 2 * P, nc.vector.tensor_copy), ("res3", acc3, 3 * P, nc.scalar.copy)):
+            width = acc.shape[1]
+            res = sbuf(name, [P, width], F32)
+            engine_copy(res[:], acc[:])
+            nc.sync.dma_start(out=out[:, col : col + width], in_=res[:])

@@ -13,7 +13,6 @@ FP8X4 = mybir.dt.float8_e4m3fn_x4
 FP4X4 = mybir.dt.float4_e2m1fn_x4
 ACT = mybir.ActivationFunctionType
 ALU = mybir.AluOpType
-AX = mybir.AxisListType
 
 P = 128
 D, T, I, Q, E, U, J = 512, 2048, 512, 128, 512, 1024, 512
@@ -44,7 +43,6 @@ def tile_attend_two_caches_kernel(tc, query, keys_words, keys_scales, rkey_words
         vpool = [sbuf("vpool%d" % k, [P, T], F32) for k in range(NB)]
         upool = [sbuf("upool%d" % k, [P, U], F32) for k in range(NB)]
         ident = sbuf("ident", [P, P], F32)
-        warm = sbuf("warm", [P, 8], F32)
 
         nc.gpsimd.memset(rs[:].bitcast(I32), 0)
         nc.gpsimd.memset(ks[:].bitcast(I32), 0)
@@ -57,10 +55,11 @@ def tile_attend_two_caches_kernel(tc, query, keys_words, keys_scales, rkey_words
         def load_rval(k):
             nc.sync.dma_start(out=upool[k][:], in_=rval[k * P : (k + 1) * P, :])
 
+        def load_vals(k):
+            nc.sync.dma_start(out=vpool[k][:], in_=vals[k * P : (k + 1) * P, :])
+
         nc.sync.dma_start(lst2[:], offs2)
         nc.sync.dma_start(out=rw[:].bitcast(I32), in_=rkey_words[0].bitcast(I32))
-        load_rval(2)
-        load_rval(3)
         nc.sync.dma_start(out=qraw[:], in_=query.rearrange("(p j) w -> p j w", j=4))
         load_scales(rs, rkey_scales, 0)
         nc.sync.dma_start(out=kw[:].bitcast(I32), in_=keys_words[0].rearrange("p n t -> p (n t)").bitcast(I32))
@@ -68,18 +67,18 @@ def tile_attend_two_caches_kernel(tc, query, keys_words, keys_scales, rkey_words
         load_scales(ks, keys_scales, 4)
         load_rval(0)
         load_rval(1)
+        load_rval(2)
         nc.sync.dma_start(out=szc[:], in_=size[0].rearrange("(p t) -> p t", t=4))
         nc.sync.dma_start(out=rszc[:], in_=rsz[0].rearrange("(p t) -> p t", t=4))
-        for k in range(NB):
-            nc.sync.dma_start(out=vpool[k][:], in_=vals[k * P : (k + 1) * P, :])
+        load_rval(3)
+        load_vals(0)
+        load_vals(1)
+        load_vals(2)
+        load_vals(3)
 
-        nc.vector.memset(warm[:], 0.0)
-        nc.scalar.activation(out=warm[:, 0:1], in_=warm[:, 4:5], func=ACT.Exp)
-
-        def turn_words(sources, dst, bank=None):
+        def turn_words(sources, dst, tag=None):
             n = len(sources)
-            if bank is None:
-                bank = turn.tile([P, n, 2, P], F32, name="bank")
+            bank = ps.tile([P, n, 2, P], F32, name="held", tag=tag) if tag else turn.tile([P, n, 2, P], F32, name="bank")
             for b, src in enumerate(sources):
                 words = src[:].bitcast(F32)
                 for u in range(2):
@@ -102,62 +101,57 @@ def tile_attend_two_caches_kernel(tc, query, keys_words, keys_scales, rkey_words
             nc.scalar.activation(out=ub[:], in_=upool[k][:], func=ACT.Copy)
             return ub
 
-        def gather_scalar(k, ub, after=None):
-            ug = sbuf("ug%d" % k, [P, J], BF16, after)
-            nc.scalar.activation(out=ug[:], in_=ub[:].indirect(lst2[:]), func=ACT.Copy)
-            return ug
-
-        def gather_vector(name, pool_tile, offsets, after=None):
+        def gather_scalar(name, window, offsets, after=None):
             picked = sbuf(name, [P, J], BF16, after)
-            nc.vector.tensor_copy(picked[:], pool_tile[:].indirect(offsets[:]))
+            nc.scalar.activation(out=picked[:], in_=window[:].indirect(offsets[:]), func=ACT.Copy)
             return picked
 
-        rwg = sbuf("rwg", [P, J], U16)
-        kwg = sbuf("kwg", [P, I], U32)
-        ksg = sbuf("ksg", [P, I], U8)
-        nc.vector.tensor_copy(rwg[:], rw[:].indirect(lst2[:]))
-        ug2 = gather_vector("ug2", upool[2], lst2)
-        ug3 = gather_scalar(3, cast_rval(3))
-        rsg = sbuf("rsg", [P, J], U8)
-        nc.vector.tensor_copy(rsg[:], rs[:].indirect(lst2[:]))
+        def gather_vector(name, window, offsets, dtype=BF16, after=None):
+            picked = sbuf(name, [P, J], dtype, after)
+            nc.vector.tensor_copy(picked[:], window[:].indirect(offsets[:]))
+            return picked
+
+        rwg = gather_vector("rwg", rw, lst2, U16)
+        rsg = gather_vector("rsg", rs, lst2, U8)
         qb = sbuf("qb", [P, Q, 4], BF16)
-        nc.vector.tensor_copy(out=qb[:], in_=qraw[:].rearrange("p j w -> p w j"))
+        nc.scalar.activation(out=qb[:], in_=qraw[:].rearrange("p j w -> p w j"), func=ACT.Copy)
         qc, qs = quantise("q", qb[:])
-        mid = sbuf("mid", [P, 4 * P, 4], BF16)
-        late = sbuf("late", [P, 4 * P, 4], BF16)
-        turn_words([ug2, ug3], mid[:, 0 : 2 * P, :], ps.tile([P, 2, 2, P], F32, name="bank23", tag="bank0"))
-        nc.vector.tensor_copy(kwg[:], kw[:].indirect(lst[:]))
-        nc.vector.tensor_copy(ksg[:], ks[:].indirect(lst[:]))
+        kwg = gather_vector("kwg", kw, lst, U32, after="rs")
+        ksg = gather_vector("ksg", ks, lst, U8)
+        first = sbuf("first", [P, 4 * P, 4], BF16)
+        second = sbuf("second", [P, 4 * P, 4], BF16)
+        tail = [sbuf("tail%d" % k, [P, P, 4], BF16) for k in range(2)]
 
         sc_b = ps.tile([P, J], F32, name="sc_b", tag="bank0")
         sc_a = ps.tile([P, I], F32, name="sc_a", tag="bank1")
         nc.tensor.matmul_mx(out=sc_b[:], lhsT=qc[:].bitcast(FP8X4), lhsT_scale=qs[:], rhs=rwg[:].bitcast(FP4X4), rhs_scale=rsg[:], start=True, stop=True)
         nc.tensor.matmul_mx(out=sc_a[:], lhsT=qc[:].bitcast(FP8X4), lhsT_scale=qs[:], rhs=kwg[:].bitcast(FP8X4), rhs_scale=ksg[4:P, :], start=True, stop=True)
-
-        spread = []
-        for name, col, tag in (("szb", szc, "bank2"), ("rszb", rszc, "bank3")):
-            bank = ps.tile([P, 4, P], F32, name=name, tag=tag)
-            for t in range(4):
-                nc.tensor.transpose(bank[:, t, :], col[:, t : t + 1].to_broadcast([P, P]), ident[:])
-            spread.append(bank)
-
-        ub0 = cast_rval(0, after="ug3")
-        ub1 = cast_rval(1)
-
-        start = sbuf("start", [P, 1], F32, after="kw")
+        start = sbuf("start", [P, 1], F32, after="ks")
         negm = sbuf("negm", [P, 1], F32)
         neg = sbuf("neg", [P, I + J], F32)
         nc.vector.tensor_scalar(out=neg[:, I : I + J], in0=sc_b[:], scalar1=-1.0, scalar2=BIG, op0=ALU.mult, op1=ALU.min, accum_out=start[:])
         nc.vector.tensor_scalar(out=neg[:, 0:I], in0=sc_a[:], scalar1=-1.0, scalar2=start[:], op0=ALU.mult, op1=ALU.min, accum_out=negm[:])
+
+        ub0 = cast_rval(0, after="qraw")
+        ub1 = cast_rval(1)
         prob = sbuf("prob", [P, I + J], F32, after="upool1")
         z = sbuf("z", [P, 1], F32)
         nc.scalar.activation(out=prob[:], in_=neg[:], func=ACT.Exp, bias=negm[:], scale=-1.0, accum_out=z[:])
+        ug0 = gather_scalar("ug0", ub0, lst2, after="neg")
+        ug1 = gather_scalar("ug1", ub1, lst2, after="negm")
 
-        ug0 = gather_scalar(0, ub0, after="neg")
-        ug1 = gather_scalar(1, ub1, after="negm")
+        spread = []
+        for name, col, tag in (("rszb", rszc, "bank0"), ("szb", szc, "bank1")):
+            bank = ps.tile([P, 4, P], F32, name=name, tag=tag)
+            for t in range(4):
+                nc.tensor.transpose(bank[:, t, :], col[:, t : t + 1].to_broadcast([P, P]), ident[:])
+            spread = [bank] + spread
 
-        vg0 = gather_vector("vg0", vpool[0], lst)
-        rz = sbuf("rz", [P, 1], F32, after="vpool0")
+        ug2 = gather_vector("ug2", upool[2], lst2, after="ks")
+        ug3 = gather_vector("ug3", upool[3], lst2, after="upool2")
+        turn_words([ug2, ug3], first[:, 2 * P : 4 * P, :])
+
+        rz = sbuf("rz", [P, 1], F32, after="upool3")
         nc.vector.reciprocal(out=rz[:], in_=z[:])
         weights = []
         for n in range(2):
@@ -171,29 +165,39 @@ def tile_attend_two_caches_kernel(tc, query, keys_words, keys_scales, rkey_words
                 op1=ALU.mult,
             )
             weights.append(weight)
-        turn_words(weights, mid[:, 2 * P : 4 * P, :])
+        turn_words([ug0, ug1], first[:, 0 : 2 * P, :])
+        turn_words(weights, second[:, 0 : 2 * P, :])
 
-        tail = [sbuf("tail%d" % k, [P, P, 4], BF16) for k in range(2)]
-        vg1 = gather_vector("vg1", vpool[1], lst)
-        turn_words([ug0, ug1], late[:, 0 : 2 * P, :], ps.tile([P, 2, 2, P], F32, name="bank01", tag="bank3"))
-        turn_words([vg0, vg1], late[:, 2 * P : 4 * P, :])
-        turn_words([gather_vector("vg2", vpool[2], lst)], tail[0][:])
-        mid_q = quantise("midq", mid[:], after="vpool2")
-        turn_words([gather_vector("vg3", vpool[3], lst)], tail[1][:])
-        late_q = quantise("lateq", late[:], after="vpool3")
-        tail_q = [quantise("tail0q", tail[0][:], after="late"), quantise("tail1q", tail[1][:])]
+        vg0 = gather_vector("vg0", vpool[0], lst, after="z")
+        vg1 = gather_vector("vg1", vpool[1], lst, after="upool3")
+        turn_words([vg0], second[:, 2 * P : 3 * P, :])
+        first_q = quantise("firstq", first[:], after="vpool0")
+        turn_words([vg1], second[:, 3 * P : 4 * P, :])
+        vg2 = gather_vector("vg2", vpool[2], lst, after="vpool1")
+        second_q = quantise("secondq", second[:], after="vpool2")
+        turn_words([vg2], tail[0][:])
 
-        acc2 = ps.tile([P, P], F32, name="acc2", tag="bank1")
-        acc3 = ps.tile([P, P], F32, name="acc3", tag="bank2")
-        acc01 = ps.tile([P, 2 * P], F32, name="acc01", tag="bank0")
-        product(acc2[:], mid_q, 3 * P, mid_q, 0, P, True, False)
-        product(acc3[:], mid_q, 3 * P, mid_q, P, P, True, False)
-        product(acc01[:], mid_q, 3 * P, late_q, 0, 2 * P, True, False)
-        product(acc01[:], mid_q, 2 * P, late_q, 2 * P, 2 * P, False, True)
-        product(acc2[:], mid_q, 2 * P, tail_q[0], 0, P, False, True)
-        product(acc3[:], mid_q, 2 * P, tail_q[1], 0, P, False, True)
-        for name, acc, col, engine_copy in (("res01", acc01, 0, nc.scalar.copy), ("res2", acc2, 2 * P, nc.vector.tensor_copy), ("res3", acc3, 3 * P, nc.scalar.copy)):
+        acc01 = ps.tile([P, 2 * P], F32, name="acc01", tag="bank2")
+        acc2 = ps.tile([P, P], F32, name="acc2", tag="bank3")
+        acc3 = ps.tile([P, P], F32, name="acc3", tag="bank0")
+
+        def store(name, acc, col, engine_copy):
             width = acc.shape[1]
             res = sbuf(name, [P, width], F32)
             engine_copy(res[:], acc[:])
             nc.sync.dma_start(out=out[:, col : col + width], in_=res[:])
+
+        vg3 = gather_vector("vg3", vpool[3], lst, after="second")
+        product(acc01[:], second_q, P, first_q, 0, 2 * P, True, False)
+        product(acc01[:], second_q, 0, second_q, 2 * P, 2 * P, False, True)
+        product(acc2[:], second_q, P, first_q, 2 * P, P, True, False)
+        product(acc3[:], second_q, P, first_q, 3 * P, P, True, False)
+        store("res01", acc01, 0, nc.scalar.copy)
+
+        tail0_q = quantise("tail0q", tail[0][:], after="vpool3")
+        turn_words([vg3], tail[1][:])
+        product(acc2[:], second_q, 0, tail0_q, 0, P, False, True)
+        tail1_q = quantise("tail1q", tail[1][:])
+        product(acc3[:], second_q, 0, tail1_q, 0, P, False, True)
+        store("res2", acc2, 2 * P, nc.vector.tensor_copy)
+        store("res3", acc3, 3 * P, nc.scalar.copy)

@@ -49,8 +49,8 @@ def tile_attend_two_caches_kernel(tc, query, keys_words, keys_scales, rkey_words
         make_identity(nc, ident[:])
 
         def load_scales(plane, scales, row):
-            for g in range(4):
-                nc.sync.dma_start(out=plane[32 * g + row : 32 * g + row + 4, :].bitcast(I32), in_=scales[0, 4 * g : 4 * g + 4, :].bitcast(I32))
+            for r in range(4):
+                nc.sync.dma_start(out=plane[row + r : P : 32, :].bitcast(I32), in_=scales[0, r : 16 : 4, :].bitcast(I32))
 
         def load_rval(k):
             nc.sync.dma_start(out=upool[k][:], in_=rval[k * P : (k + 1) * P, :])
@@ -142,9 +142,9 @@ def tile_attend_two_caches_kernel(tc, query, keys_words, keys_scales, rkey_words
 
         spread = []
         for name, col, tag in (("rszb", rszc, "bank0"), ("szb", szc, "bank1")):
-            bank = ps.tile([P, 4, P], F32, name=name, tag=tag)
+            bank = ps.tile([P, P, 4], F32, name=name, tag=tag)
             for t in range(4):
-                nc.tensor.transpose(bank[:, t, :], col[:, t : t + 1].to_broadcast([P, P]), ident[:])
+                nc.tensor.transpose(bank[:, :, t], col[:, t : t + 1].to_broadcast([P, P]), ident[:])
             spread = [bank] + spread
 
         ug2 = gather_vector("ug2", upool[2], lst2, after="ks")
@@ -157,10 +157,10 @@ def tile_attend_two_caches_kernel(tc, query, keys_words, keys_scales, rkey_words
         for n in range(2):
             weight = sbuf("weight%d" % n, [P, I], BF16)
             nc.vector.scalar_tensor_tensor(
-                out=weight[:].rearrange("q (s t) -> q s t", t=4),
-                in0=prob[:, n * I : (n + 1) * I].rearrange("q (s t) -> q s t", t=4),
+                out=weight[:],
+                in0=prob[:, n * I : (n + 1) * I],
                 scalar=rz[:],
-                in1=spread[n][:].rearrange("q t s -> q s t"),
+                in1=spread[n][:].rearrange("q s t -> q (s t)"),
                 op0=ALU.mult,
                 op1=ALU.mult,
             )

@@ -65,12 +65,12 @@ def tile_attend_two_caches_kernel(tc, query, keys_words, keys_scales, rkey_words
         nc.sync.dma_start(out=kw[:].bitcast(I32), in_=keys_words[0].rearrange("p n t -> p (n t)").bitcast(I32))
         nc.sync.dma_start(lst[:], offs)
         load_scales(ks, keys_scales, 4)
-        load_rval(0)
-        load_rval(1)
         load_rval(2)
+        load_rval(0)
+        load_rval(3)
         nc.sync.dma_start(out=szc[:], in_=size[0].rearrange("(p t) -> p t", t=4))
         nc.sync.dma_start(out=rszc[:], in_=rsz[0].rearrange("(p t) -> p t", t=4))
-        load_rval(3)
+        load_rval(1)
         load_vals(0)
         load_vals(1)
         load_vals(2)
@@ -118,9 +118,6 @@ def tile_attend_two_caches_kernel(tc, query, keys_words, keys_scales, rkey_words
         qc, qs = quantise("q", qb[:])
         kwg = gather_vector("kwg", kw, lst, U32, after="rs")
         ksg = gather_vector("ksg", ks, lst, U8)
-        first = sbuf("first", [P, 4 * P, 4], BF16)
-        second = sbuf("second", [P, 4 * P, 4], BF16)
-        tail = [sbuf("tail%d" % k, [P, P, 4], BF16) for k in range(2)]
 
         sc_b = ps.tile([P, J], F32, name="sc_b", tag="bank0")
         sc_a = ps.tile([P, I], F32, name="sc_a", tag="bank1")
@@ -132,13 +129,10 @@ def tile_attend_two_caches_kernel(tc, query, keys_words, keys_scales, rkey_words
         nc.vector.tensor_scalar(out=neg[:, I : I + J], in0=sc_b[:], scalar1=-1.0, scalar2=BIG, op0=ALU.mult, op1=ALU.min, accum_out=start[:])
         nc.vector.tensor_scalar(out=neg[:, 0:I], in0=sc_a[:], scalar1=-1.0, scalar2=start[:], op0=ALU.mult, op1=ALU.min, accum_out=negm[:])
 
-        ub0 = cast_rval(0, after="qraw")
-        ub1 = cast_rval(1)
-        prob = sbuf("prob", [P, I + J], F32, after="upool1")
+        ug2 = gather_scalar("ug2", cast_rval(2, after="qraw"), lst2)
+        prob = sbuf("prob", [P, I + J], F32, after="qraw")
         z = sbuf("z", [P, 1], F32)
         nc.scalar.activation(out=prob[:], in_=neg[:], func=ACT.Exp, bias=negm[:], scale=-1.0, accum_out=z[:])
-        ug0 = gather_scalar("ug0", ub0, lst2, after="neg")
-        ug1 = gather_scalar("ug1", ub1, lst2, after="negm")
 
         spread = []
         for name, col, tag in (("rszb", rszc, "bank0"), ("szb", szc, "bank1")):
@@ -147,11 +141,17 @@ def tile_attend_two_caches_kernel(tc, query, keys_words, keys_scales, rkey_words
                 nc.tensor.transpose(bank[:, :, t], col[:, t : t + 1].to_broadcast([P, P]), ident[:])
             spread = [bank] + spread
 
-        ug2 = gather_vector("ug2", upool[2], lst2, after="ks")
-        ug3 = gather_vector("ug3", upool[3], lst2, after="upool2")
-        turn_words([ug2, ug3], first[:, 2 * P : 4 * P, :])
+        ug3 = gather_vector("ug3", upool[3], lst2, after="ks")
+        early = sbuf("early", [P, 2 * P, 4], BF16, after="neg")
+        middle = sbuf("middle", [P, 4 * P, 4], BF16)
+        late = sbuf("late", [P, 2 * P, 4], BF16)
+        tail = [sbuf("tail%d" % k, [P, P, 4], BF16) for k in range(2)]
+        turn_words([ug2, ug3], early[:])
+        ub0 = cast_rval(0, after="negm")
+        ug0 = gather_scalar("ug0", ub0, lst2)
+        ub1 = cast_rval(1, after="negm")
 
-        rz = sbuf("rz", [P, 1], F32, after="upool3")
+        rz = sbuf("rz", [P, 1], F32)
         nc.vector.reciprocal(out=rz[:], in_=z[:])
         weights = []
         for n in range(2):
@@ -165,20 +165,21 @@ def tile_attend_two_caches_kernel(tc, query, keys_words, keys_scales, rkey_words
                 op1=ALU.mult,
             )
             weights.append(weight)
-        turn_words([ug0, ug1], first[:, 0 : 2 * P, :])
-        turn_words(weights, second[:, 0 : 2 * P, :])
+        turn_words(weights, middle[:, 0 : 2 * P, :])
+        early_q = quantise("earlyq", early[:])
 
         vg0 = gather_vector("vg0", vpool[0], lst, after="z")
-        vg1 = gather_vector("vg1", vpool[1], lst, after="upool3")
-        turn_words([vg0], second[:, 2 * P : 3 * P, :])
-        first_q = quantise("firstq", first[:], after="vpool0")
-        turn_words([vg1], second[:, 3 * P : 4 * P, :])
-        vg2 = gather_vector("vg2", vpool[2], lst, after="vpool1")
-        second_q = quantise("secondq", second[:], after="vpool2")
+        vg1 = gather_vector("vg1", vpool[1], lst, after="rz")
+        turn_words([ug0, vg0], middle[:, 2 * P : 4 * P, :])
+        turn_words([vg1], late[:, P : 2 * P, :])
+        ug1 = gather_scalar("ug1", ub1, lst2, after="rz")
+        vg2 = gather_vector("vg2", vpool[2], lst, after="vpool0")
+        middle_q = quantise("middleq", middle[:], after="vpool2")
         turn_words([vg2], tail[0][:])
+        turn_words([ug1], late[:, 0:P, :])
 
-        acc01 = ps.tile([P, 2 * P], F32, name="acc01", tag="bank2")
-        acc2 = ps.tile([P, P], F32, name="acc2", tag="bank3")
+        acc0 = ps.tile([P, P], F32, name="acc0", tag="bank2")
+        acc12 = ps.tile([P, 2 * P], F32, name="acc12", tag="bank3")
         acc3 = ps.tile([P, P], F32, name="acc3", tag="bank0")
 
         def store(name, acc, col, engine_copy):
@@ -187,17 +188,20 @@ def tile_attend_two_caches_kernel(tc, query, keys_words, keys_scales, rkey_words
             engine_copy(res[:], acc[:])
             nc.sync.dma_start(out=out[:, col : col + width], in_=res[:])
 
-        vg3 = gather_vector("vg3", vpool[3], lst, after="second")
-        product(acc01[:], second_q, P, first_q, 0, 2 * P, True, False)
-        product(acc01[:], second_q, 0, second_q, 2 * P, 2 * P, False, True)
-        product(acc2[:], second_q, P, first_q, 2 * P, P, True, False)
-        product(acc3[:], second_q, P, first_q, 3 * P, P, True, False)
-        store("res01", acc01, 0, nc.scalar.copy)
+        vg3 = gather_vector("vg3", vpool[3], lst, after="middle")
+        product(acc0[:], middle_q, P, middle_q, 2 * P, P, True, False)
+        product(acc0[:], middle_q, 0, middle_q, 3 * P, P, False, True)
+        product(acc3[:], middle_q, P, early_q, P, P, True, False)
+        product(acc12[:, P : 2 * P], middle_q, P, early_q, 0, P, True, False)
+        store("res0", acc0, 0, nc.scalar.copy)
 
         tail0_q = quantise("tail0q", tail[0][:], after="vpool3")
         turn_words([vg3], tail[1][:])
-        product(acc2[:], second_q, 0, tail0_q, 0, P, False, True)
+        late_q = quantise("lateq", late[:], after="tail0")
+        product(acc12[:, P : 2 * P], middle_q, 0, tail0_q, 0, P, False, True)
+        product(acc12[:, 0:P], middle_q, P, late_q, 0, P, True, False)
+        product(acc12[:, 0:P], middle_q, 0, late_q, P, P, False, True)
         tail1_q = quantise("tail1q", tail[1][:])
-        product(acc3[:], second_q, 0, tail1_q, 0, P, False, True)
-        store("res2", acc2, 2 * P, nc.vector.tensor_copy)
-        store("res3", acc3, 3 * P, nc.scalar.copy)
+        product(acc3[:], middle_q, 0, tail1_q, 0, P, False, True)
+        store("res12", acc12, P, nc.scalar.copy)
+        store("res3", acc3, 3 * P, nc.vector.tensor_copy)

@@ -41,16 +41,17 @@ def tile_attend_two_caches_kernel(tc, query, keys_words, keys_scales, rkey_words
         szc = sbuf("szc", [P, 4], F32)
         rszc = sbuf("rszc", [P, 4], F32)
         vpool = [sbuf("vpool%d" % k, [P, T], F32) for k in range(NB)]
-        upool = [sbuf("upool%d" % k, [P, U], F32) for k in range(NB)]
+        upair = sbuf("upair", [P, 2, U], F32)
+        upool = [upair[:, 0, :], upair[:, 1, :]] + [sbuf("upool%d" % k, [P, U], F32) for k in (2, 3)]
         ident = sbuf("ident", [P, P], F32)
 
         nc.gpsimd.memset(rs[:].bitcast(I32), 0)
         nc.gpsimd.memset(ks[:].bitcast(I32), 0)
         make_identity(nc, ident[:])
 
-        def load_scales(plane, scales, row):
+        def load_scales(plane, scales, row, queue):
             for r in range(4):
-                nc.sync.dma_start(out=plane[row + r : P : 32, :].bitcast(I32), in_=scales[0, r : 16 : 4, :].bitcast(I32))
+                queue.dma_start(out=plane[row + r : P : 32, :].bitcast(I32), in_=scales[0, r : 16 : 4, :].bitcast(I32))
 
         def load_rval(k):
             nc.sync.dma_start(out=upool[k][:], in_=rval[k * P : (k + 1) * P, :])
@@ -58,23 +59,22 @@ def tile_attend_two_caches_kernel(tc, query, keys_words, keys_scales, rkey_words
         def load_vals(k):
             nc.sync.dma_start(out=vpool[k][:], in_=vals[k * P : (k + 1) * P, :])
 
-        nc.sync.dma_start(lst2[:], offs2)
         nc.sync.dma_start(out=rw[:].bitcast(I32), in_=rkey_words[0].bitcast(I32))
+        nc.sync.dma_start(lst2[:], offs2)
         nc.sync.dma_start(out=qraw[:], in_=query.rearrange("(p j) w -> p j w", j=4))
-        load_scales(rs, rkey_scales, 0)
+        load_scales(rs, rkey_scales, 0, nc.sync)
         nc.sync.dma_start(out=kw[:].bitcast(I32), in_=keys_words[0].rearrange("p n t -> p (n t)").bitcast(I32))
         nc.sync.dma_start(lst[:], offs)
-        load_scales(ks, keys_scales, 4)
+        load_scales(ks, keys_scales, 4, nc.sync)
         load_rval(2)
-        load_rval(0)
         load_rval(3)
-        nc.sync.dma_start(out=szc[:], in_=size[0].rearrange("(p t) -> p t", t=4))
-        nc.sync.dma_start(out=rszc[:], in_=rsz[0].rearrange("(p t) -> p t", t=4))
-        load_rval(1)
+        nc.sync.dma_start(out=upair[:], in_=rval[0 : 2 * P, :].rearrange("(k p) u -> p k u", p=P))
         load_vals(0)
         load_vals(1)
         load_vals(2)
         load_vals(3)
+        nc.gpsimd.dma_start(out=szc[:], in_=size[0].rearrange("(p t) -> p t", t=4))
+        nc.gpsimd.dma_start(out=rszc[:], in_=rsz[0].rearrange("(p t) -> p t", t=4))
 
         def turn_words(sources, dst, tag=None):
             n = len(sources)
@@ -129,17 +129,17 @@ def tile_attend_two_caches_kernel(tc, query, keys_words, keys_scales, rkey_words
         nc.vector.tensor_scalar(out=neg[:, I : I + J], in0=sc_b[:], scalar1=-1.0, scalar2=BIG, op0=ALU.mult, op1=ALU.min, accum_out=start[:])
         nc.vector.tensor_scalar(out=neg[:, 0:I], in0=sc_a[:], scalar1=-1.0, scalar2=start[:], op0=ALU.mult, op1=ALU.min, accum_out=negm[:])
 
-        ug2 = gather_scalar("ug2", cast_rval(2, after="qraw"), lst2)
+        ug2 = gather_scalar("ug2", cast_rval(2, after="qraw"), lst2, after="rs")
         prob = sbuf("prob", [P, I + J], F32, after="qraw")
         z = sbuf("z", [P, 1], F32)
         nc.scalar.activation(out=prob[:], in_=neg[:], func=ACT.Exp, bias=negm[:], scale=-1.0, accum_out=z[:])
 
         spread = []
-        for name, col, tag in (("rszb", rszc, "bank0"), ("szb", szc, "bank1")):
+        for name, col, tag in (("szb", szc, "bank0"), ("rszb", rszc, "bank1")):
             bank = ps.tile([P, P, 4], F32, name=name, tag=tag)
             for t in range(4):
                 nc.tensor.transpose(bank[:, :, t], col[:, t : t + 1].to_broadcast([P, P]), ident[:])
-            spread = [bank] + spread
+            spread.append(bank)
 
         ug3 = gather_vector("ug3", upool[3], lst2, after="ks")
         early = sbuf("early", [P, 2 * P, 4], BF16, after="neg")
@@ -182,13 +182,13 @@ def tile_attend_two_caches_kernel(tc, query, keys_words, keys_scales, rkey_words
         acc12 = ps.tile([P, 2 * P], F32, name="acc12", tag="bank3")
         acc3 = ps.tile([P, P], F32, name="acc3", tag="bank0")
 
-        def store(name, acc, col, engine_copy):
+        def store(name, acc, col, engine_copy, queue=nc.sync):
             width = acc.shape[1]
             res = sbuf(name, [P, width], F32)
             engine_copy(res[:], acc[:])
-            nc.sync.dma_start(out=out[:, col : col + width], in_=res[:])
+            queue.dma_start(out=out[:, col : col + width], in_=res[:])
 
-        vg3 = gather_vector("vg3", vpool[3], lst, after="middle")
+        vg3 = gather_vector("vg3", vpool[3], lst, after="vpool0")
         product(acc0[:], middle_q, P, middle_q, 2 * P, P, True, False)
         product(acc0[:], middle_q, 0, middle_q, 3 * P, P, False, True)
         product(acc3[:], middle_q, P, early_q, P, P, True, False)
@@ -203,5 +203,5 @@ def tile_attend_two_caches_kernel(tc, query, keys_words, keys_scales, rkey_words
         product(acc12[:, 0:P], middle_q, 0, late_q, P, P, False, True)
         tail1_q = quantise("tail1q", tail[1][:])
         product(acc3[:], middle_q, 0, tail1_q, 0, P, False, True)
-        store("res12", acc12, P, nc.scalar.copy)
-        store("res3", acc3, 3 * P, nc.vector.tensor_copy)
+        store("res12", acc12, P, nc.vector.tensor_copy)
+        store("res3", acc3, 3 * P, nc.scalar.copy, nc.scalar)

@@ -136,9 +136,9 @@ def tile_attend_two_caches_kernel(tc, query, keys_words, keys_scales, rkey_words
 
         spread = []
         for name, col, tag in (("szb", szc, "bank0"), ("rszb", rszc, "bank1")):
-            bank = ps.tile([P, P, 4], F32, name=name, tag=tag)
+            bank = ps.tile([P, 4, P], F32, name=name, tag=tag)
             for t in range(4):
-                nc.tensor.transpose(bank[:, :, t], col[:, t : t + 1].to_broadcast([P, P]), ident[:])
+                nc.tensor.transpose(bank[:, t, :], col[:, t : t + 1].to_broadcast([P, P]), ident[:])
             spread.append(bank)
 
         ug3 = gather_vector("ug3", upool[3], lst2, after="ks")
@@ -157,10 +157,10 @@ def tile_attend_two_caches_kernel(tc, query, keys_words, keys_scales, rkey_words
         for n in range(2):
             weight = sbuf("weight%d" % n, [P, I], BF16)
             nc.vector.scalar_tensor_tensor(
-                out=weight[:],
-                in0=prob[:, n * I : (n + 1) * I],
+                out=weight[:].rearrange("q (s t) -> q s t", t=4),
+                in0=prob[:, n * I : (n + 1) * I].rearrange("q (s t) -> q s t", t=4),
                 scalar=rz[:],
-                in1=spread[n][:].rearrange("q s t -> q (s t)"),
+                in1=spread[n][:].rearrange("q t s -> q s t"),
                 op0=ALU.mult,
                 op1=ALU.mult,
             )

@@ -26,7 +26,6 @@ def tile_attend_two_caches_kernel(tc, query, keys_words, keys_scales, rkey_words
     with ExitStack() as ctx:
         sb = ctx.enter_context(tc.tile_pool(name="sb", bufs=1))
         ps = ctx.enter_context(tc.psum_pool(name="ps", bufs=1))
-        turn = ctx.enter_context(tc.psum_pool(name="turn", bufs=4))
 
         def sbuf(name, shape, dtype, after=None):
             return sb.tile(shape, dtype, name=name, tag=after or name, align_bytes=64)
@@ -41,83 +40,85 @@ def tile_attend_two_caches_kernel(tc, query, keys_words, keys_scales, rkey_words
         szc = sbuf("szc", [P, 4], F32)
         rszc = sbuf("rszc", [P, 4], F32)
         vpool = [sbuf("vpool%d" % k, [P, T], F32) for k in range(NB)]
-        upair = sbuf("upair", [P, 2, U], F32)
-        upool = [upair[:, 0, :], upair[:, 1, :]] + [sbuf("upool%d" % k, [P, U], F32) for k in (2, 3)]
+        upool = [sbuf("upool%d" % k, [P, U], F32) for k in range(NB)]
         ident = sbuf("ident", [P, P], F32)
 
-        nc.gpsimd.memset(rs[:].bitcast(I32), 0)
-        nc.gpsimd.memset(ks[:].bitcast(I32), 0)
+        nc.gpsimd.dma_start(out=szc[:], in_=size[0].rearrange("(p t) -> p t", t=4))
+        nc.gpsimd.dma_start(out=rszc[:], in_=rsz[0].rearrange("(p t) -> p t", t=4))
+        nc.vector.memset(rs[:].bitcast(I32), 0)
+        nc.vector.memset(ks[:].bitcast(I32), 0)
         make_identity(nc, ident[:])
 
-        def load_scales(plane, scales, row, queue):
+        def load_scales(plane, scales, row):
             for r in range(4):
-                queue.dma_start(out=plane[row + r : P : 32, :].bitcast(I32), in_=scales[0, r : 16 : 4, :].bitcast(I32))
+                nc.sync.dma_start(out=plane[row + r : P : 32, :].bitcast(I32), in_=scales[0, r : 16 : 4, :].bitcast(I32))
+
+        nc.sync.dma_start(out=rw[:].bitcast(I32), in_=rkey_words[0].bitcast(I32))
+        nc.sync.dma_start(lst2[:], offs2)
+        nc.sync.dma_start(lst[:], offs)
+        load_scales(rs, rkey_scales, 0)
+        nc.sync.dma_start(out=kw[:].bitcast(I32), in_=keys_words[0].rearrange("p n t -> p (n t)").bitcast(I32))
+        nc.sync.dma_start(out=qraw[:], in_=query.rearrange("(p j) w -> p j w", j=4))
+        load_scales(ks, keys_scales, 4)
 
         def load_rval(k):
             nc.sync.dma_start(out=upool[k][:], in_=rval[k * P : (k + 1) * P, :])
 
-        def load_vals(k):
+        for k in range(NB):
+            load_rval(k)
+        for k in range(NB):
             nc.sync.dma_start(out=vpool[k][:], in_=vals[k * P : (k + 1) * P, :])
 
-        nc.sync.dma_start(out=rw[:].bitcast(I32), in_=rkey_words[0].bitcast(I32))
-        nc.sync.dma_start(lst2[:], offs2)
-        nc.sync.dma_start(out=qraw[:], in_=query.rearrange("(p j) w -> p j w", j=4))
-        load_scales(rs, rkey_scales, 0, nc.sync)
-        nc.sync.dma_start(out=kw[:].bitcast(I32), in_=keys_words[0].rearrange("p n t -> p (n t)").bitcast(I32))
-        nc.sync.dma_start(lst[:], offs)
-        load_scales(ks, keys_scales, 4, nc.sync)
-        load_rval(2)
-        load_rval(3)
-        nc.sync.dma_start(out=upair[:], in_=rval[0 : 2 * P, :].rearrange("(k p) u -> p k u", p=P))
-        load_vals(0)
-        load_vals(1)
-        load_vals(2)
-        load_vals(3)
-        nc.gpsimd.dma_start(out=szc[:], in_=size[0].rearrange("(p t) -> p t", t=4))
-        nc.gpsimd.dma_start(out=rszc[:], in_=rsz[0].rearrange("(p t) -> p t", t=4))
+        def in_order(picked):
+            words = picked.bitcast(F32)
+            return [words[:, u : 2 * P : 2] for u in range(2)]
 
-        def turn_words(sources, dst, tag=None):
+        def turn_words(sources, dst, tag, engine_copy=nc.scalar.copy):
             n = len(sources)
-            bank = ps.tile([P, n, 2, P], F32, name="held", tag=tag) if tag else turn.tile([P, n, 2, P], F32, name="bank")
-            for b, src in enumerate(sources):
-                words = src[:].bitcast(F32)
+            bank = ps.tile([P, n, 2, P], F32, name="turned", tag=tag)
+            for b, halves in enumerate(sources):
                 for u in range(2):
-                    nc.tensor.transpose(bank[:, b, u, :], words[:, u : 2 * P : 2], ident[:])
-            nc.scalar.copy(out=dst.bitcast(F32).rearrange("p (b r) u -> p b r u", b=n), in_=bank[:].rearrange("p b u r -> p b r u"))
+                    nc.tensor.transpose(bank[:, b, u, :], halves[u], ident[:])
+            engine_copy(dst.bitcast(F32).rearrange("p (b r u) -> p b r u", b=n, u=2), bank[:].rearrange("p b u r -> p b r u"))
 
         def quantise(name, src, after=None):
-            cols = src.shape[1]
+            cols = src.shape[1] // 4
             codes = sbuf(name + "c", [P, cols], U32, after)
             plane = sbuf(name + "s", [P, cols], U8)
-            nc.vector.quantize_mx(out=codes[:].bitcast(FP8X4), scales=plane[:], in_=src.rearrange("p e t -> p (e t)"))
+            nc.vector.quantize_mx(out=codes[:].bitcast(FP8X4), scales=plane[:], in_=src)
             return codes, plane
 
-        def product(dst, left, lcol, right, rcol, width, start, stop):
-            lc, rc = slice(lcol, lcol + P), slice(rcol, rcol + width)
+        def product(dst, left, lcol, right, rcol, start, stop):
+            lc, rc = slice(lcol, lcol + P), slice(rcol, rcol + P)
             nc.tensor.matmul_mx(out=dst, lhsT=left[0][:, lc].bitcast(FP8X4), lhsT_scale=left[1][:, lc], rhs=right[0][:, rc].bitcast(FP8X4), rhs_scale=right[1][:, rc], start=start, stop=stop)
 
-        def cast_rval(k, after=None):
-            ub = sbuf("ub%d" % k, [P, U], BF16, after)
-            nc.scalar.activation(out=ub[:], in_=upool[k][:], func=ACT.Copy)
-            return ub
+        def gather_packed(name, window, offsets, dtype):
+            picked = sbuf(name, [P, J], dtype)
+            nc.vector.tensor_copy(picked[:], window[:].indirect(offsets[:]))
+            return picked
 
         def gather_scalar(name, window, offsets, after=None):
             picked = sbuf(name, [P, J], BF16, after)
             nc.scalar.activation(out=picked[:], in_=window[:].indirect(offsets[:]), func=ACT.Copy)
-            return picked
+            return in_order(picked[:])
 
-        def gather_vector(name, window, offsets, dtype=BF16, after=None):
-            picked = sbuf(name, [P, J], dtype, after)
+        def gather_vector(name, window, offsets, after=None):
+            picked = sbuf(name, [P, J], BF16, after)
             nc.vector.tensor_copy(picked[:], window[:].indirect(offsets[:]))
-            return picked
+            return in_order(picked[:])
 
-        rwg = gather_vector("rwg", rw, lst2, U16)
-        rsg = gather_vector("rsg", rs, lst2, U8)
+        def gather_halves(picked, window):
+            nc.vector.tensor_copy(picked[:, 0 : I // 2], window[:].indirect(lst[:, 0 : I // 32]))
+            nc.scalar.activation(out=picked[:, I // 2 : I], in_=window[:].indirect(lst[:, I // 32 : I // 16]), func=ACT.Copy)
+            return in_order(picked)
+
+        rwg = gather_packed("rwg", rw, lst2, U16)
+        rsg = gather_packed("rsg", rs, lst2, U8)
+        kwg = gather_packed("kwg", kw, lst, U32)
         qb = sbuf("qb", [P, Q, 4], BF16)
         nc.scalar.activation(out=qb[:], in_=qraw[:].rearrange("p j w -> p w j"), func=ACT.Copy)
-        qc, qs = quantise("q", qb[:])
-        kwg = gather_vector("kwg", kw, lst, U32, after="rs")
-        ksg = gather_vector("ksg", ks, lst, U8)
+        qc, qs = quantise("q", qb[:].rearrange("p w j -> p (w j)"))
+        ksg = gather_packed("ksg", ks, lst, U8)
 
         sc_b = ps.tile([P, J], F32, name="sc_b", tag="bank0")
         sc_a = ps.tile([P, I], F32, name="sc_a", tag="bank1")
@@ -129,29 +130,25 @@ def tile_attend_two_caches_kernel(tc, query, keys_words, keys_scales, rkey_words
         nc.vector.tensor_scalar(out=neg[:, I : I + J], in0=sc_b[:], scalar1=-1.0, scalar2=BIG, op0=ALU.mult, op1=ALU.min, accum_out=start[:])
         nc.vector.tensor_scalar(out=neg[:, 0:I], in0=sc_a[:], scalar1=-1.0, scalar2=start[:], op0=ALU.mult, op1=ALU.min, accum_out=negm[:])
 
-        ug2 = gather_scalar("ug2", cast_rval(2, after="qraw"), lst2, after="rs")
-        prob = sbuf("prob", [P, I + J], F32, after="qraw")
+        ug0 = gather_scalar("ug0", upool[0], lst2)
+        ug1 = gather_scalar("ug1", upool[1], lst2)
+        prob = sbuf("prob", [P, I + J], F32, after="upool1")
         z = sbuf("z", [P, 1], F32)
         nc.scalar.activation(out=prob[:], in_=neg[:], func=ACT.Exp, bias=negm[:], scale=-1.0, accum_out=z[:])
 
         spread = []
-        for name, col, tag in (("szb", szc, "bank0"), ("rszb", rszc, "bank1")):
+        for name, col, tag in (("szb", szc, "bank2"), ("rszb", rszc, "bank3")):
             bank = ps.tile([P, 4, P], F32, name=name, tag=tag)
             for t in range(4):
                 nc.tensor.transpose(bank[:, t, :], col[:, t : t + 1].to_broadcast([P, P]), ident[:])
             spread.append(bank)
 
-        ug3 = gather_vector("ug3", upool[3], lst2, after="ks")
-        early = sbuf("early", [P, 2 * P, 4], BF16, after="neg")
-        middle = sbuf("middle", [P, 4 * P, 4], BF16)
-        late = sbuf("late", [P, 2 * P, 4], BF16)
-        tail = [sbuf("tail%d" % k, [P, P, 4], BF16) for k in range(2)]
-        turn_words([ug2, ug3], early[:])
-        ub0 = cast_rval(0, after="negm")
-        ug0 = gather_scalar("ug0", ub0, lst2)
-        ub1 = cast_rval(1, after="negm")
+        ug2 = gather_vector("ug2", upool[2], lst2, after="ks")
+        ug3 = gather_scalar("ug3", upool[3], lst2, after="neg")
+        low = sbuf("low", [P, 8 * P], BF16, after="negm")
+        turn_words([ug0, ug1], low[:], "bank0")
 
-        rz = sbuf("rz", [P, 1], F32)
+        rz = sbuf("rz", [P, 1], F32, after="upool2")
         nc.vector.reciprocal(out=rz[:], in_=z[:])
         weights = []
         for n in range(2):
@@ -164,44 +161,52 @@ def tile_attend_two_caches_kernel(tc, query, keys_words, keys_scales, rkey_words
                 op0=ALU.mult,
                 op1=ALU.mult,
             )
-            weights.append(weight)
-        turn_words(weights, middle[:, 0 : 2 * P, :])
-        early_q = quantise("earlyq", early[:])
+            weights.append(in_order(weight[:]))
+        vg0 = gather_scalar("vg0", vpool[0], lst, after="upool3")
+        low_q = quantise("lowq", low[:])
+        mid = sbuf("mid", [P, 16 * P], BF16)
+        turn_words([ug2, ug3], mid[:, 0 : 8 * P], "bank1", nc.vector.tensor_copy)
+        turn_words(weights, mid[:, 8 * P : 16 * P], "bank6", nc.vector.tensor_copy)
+        vg1 = gather_scalar("vg1", vpool[1], lst)
 
-        vg0 = gather_vector("vg0", vpool[0], lst, after="z")
-        vg1 = gather_vector("vg1", vpool[1], lst, after="rz")
-        turn_words([ug0, vg0], middle[:, 2 * P : 4 * P, :])
-        turn_words([vg1], late[:, P : 2 * P, :])
-        ug1 = gather_scalar("ug1", ub1, lst2, after="rz")
-        vg2 = gather_vector("vg2", vpool[2], lst, after="vpool0")
-        middle_q = quantise("middleq", middle[:], after="vpool2")
-        turn_words([vg2], tail[0][:])
-        turn_words([ug1], late[:, 0:P, :])
+        def turn_block(k, vg, tag, engine_copy, after=None):
+            vt = sbuf("vt%d" % k, [P, 4 * P], BF16, after)
+            turn_words([vg], vt[:], tag, engine_copy)
+            return vt
 
-        acc0 = ps.tile([P, P], F32, name="acc0", tag="bank2")
-        acc12 = ps.tile([P, 2 * P], F32, name="acc12", tag="bank3")
-        acc3 = ps.tile([P, P], F32, name="acc3", tag="bank0")
+        vt0 = turn_block(0, vg0, "bank7", nc.vector.tensor_copy)
+        mid_q = quantise("midq", mid[:])
+        recent = [(low_q, 0), (low_q, P), (mid_q, 0), (mid_q, P)]
+        w_col, x_col = 2 * P, 3 * P
 
-        def store(name, acc, col, engine_copy, queue=nc.sync):
-            width = acc.shape[1]
-            res = sbuf(name, [P, width], F32)
-            engine_copy(res[:], acc[:])
+        front = ps.tile([P, 2 * P], F32, name="front", tag="bank4")
+        third = ps.tile([P, P], F32, name="third", tag="bank1")
+        last = ps.tile([P, P], F32, name="last", tag="bank5")
+        acc = [front[:, 0:P], front[:, P : 2 * P], third[:], last[:]]
+        for k in (2, 3):
+            product(acc[k], mid_q, x_col, recent[k][0], recent[k][1], True, False)
+
+        def finish(k, turned, after=None):
+            vq = quantise("vq%d" % k, turned[:], after)
+            if k < 2:
+                product(acc[k], mid_q, x_col, recent[k][0], recent[k][1], True, False)
+            product(acc[k], mid_q, w_col, vq, 0, False, True)
+
+        def store(name, bank, col, engine_copy, queue, after=None):
+            width = bank.shape[1]
+            res = sbuf(name, [P, width], F32, after)
+            engine_copy(res[:], bank[:])
             queue.dma_start(out=out[:, col : col + width], in_=res[:])
 
-        vg3 = gather_vector("vg3", vpool[3], lst, after="vpool0")
-        product(acc0[:], middle_q, P, middle_q, 2 * P, P, True, False)
-        product(acc0[:], middle_q, 0, middle_q, 3 * P, P, False, True)
-        product(acc3[:], middle_q, P, early_q, P, P, True, False)
-        product(acc12[:, P : 2 * P], middle_q, P, early_q, 0, P, True, False)
-        store("res0", acc0, 0, nc.scalar.copy)
-
-        tail0_q = quantise("tail0q", tail[0][:], after="vpool3")
-        turn_words([vg3], tail[1][:])
-        late_q = quantise("lateq", late[:], after="tail0")
-        product(acc12[:, P : 2 * P], middle_q, 0, tail0_q, 0, P, False, True)
-        product(acc12[:, 0:P], middle_q, P, late_q, 0, P, True, False)
-        product(acc12[:, 0:P], middle_q, 0, late_q, P, P, False, True)
-        tail1_q = quantise("tail1q", tail[1][:])
-        product(acc3[:], middle_q, 0, tail1_q, 0, P, False, True)
-        store("res12", acc12, P, nc.vector.tensor_copy)
-        store("res3", acc3, 3 * P, nc.scalar.copy, nc.scalar)
+        finish(0, vt0)
+        vt1 = turn_block(1, vg1, "bank2", nc.scalar.copy)
+        vg2 = gather_vector("vg2", vpool[2], lst, after="vt0")
+        finish(1, vt1, after="vpool2")
+        vg3 = gather_halves(vt1[:], vpool[3])
+        vt2 = turn_block(2, vg2, "bank3", nc.scalar.copy, after="vpool3")
+        vt3 = turn_block(3, vg3, "bank0", nc.scalar.copy)
+        store("res_front", front, 0, nc.vector.tensor_copy, nc.sync, after="vt1")
+        finish(2, vt2)
+        finish(3, vt3)
+        store("res_third", third, 2 * P, nc.vector.tensor_copy, nc.sync, after="vt3")
+        store("res_last", last, 3 * P, nc.scalar.copy, nc.scalar)

@@ -145,8 +145,6 @@ def tile_attend_two_caches_kernel(tc, query, keys_words, keys_scales, rkey_words
 
         ug2 = gather_vector("ug2", upool[2], lst2, after="ks")
         ug3 = gather_scalar("ug3", upool[3], lst2, after="neg")
-        low = sbuf("low", [P, 8 * P], BF16, after="negm")
-        turn_words([ug0, ug1], low[:], "bank0")
 
         rz = sbuf("rz", [P, 1], F32, after="upool2")
         nc.vector.reciprocal(out=rz[:], in_=z[:])
@@ -163,11 +161,13 @@ def tile_attend_two_caches_kernel(tc, query, keys_words, keys_scales, rkey_words
             )
             weights.append(in_order(weight[:]))
         vg0 = gather_scalar("vg0", vpool[0], lst, after="upool3")
+        low = sbuf("low", [P, 8 * P], BF16, after="upool2")
+        turn_words([ug0, ug1], low[:], "bank0", nc.vector.tensor_copy)
         low_q = quantise("lowq", low[:])
         mid = sbuf("mid", [P, 16 * P], BF16)
         turn_words([ug2, ug3], mid[:, 0 : 8 * P], "bank1", nc.vector.tensor_copy)
         turn_words(weights, mid[:, 8 * P : 16 * P], "bank6", nc.vector.tensor_copy)
-        vg1 = gather_scalar("vg1", vpool[1], lst)
+        vg1 = gather_scalar("vg1", vpool[1], lst, after="vpool0")
 
         def turn_block(k, vg, tag, engine_copy, after=None):
             vt = sbuf("vt%d" % k, [P, 4 * P], BF16, after)
@@ -199,9 +199,9 @@ def tile_attend_two_caches_kernel(tc, query, keys_words, keys_scales, rkey_words
             queue.dma_start(out=out[:, col : col + width], in_=res[:])
 
         finish(0, vt0)
-        vt1 = turn_block(1, vg1, "bank2", nc.scalar.copy)
-        vg2 = gather_vector("vg2", vpool[2], lst, after="vt0")
-        finish(1, vt1, after="vpool2")
+        vt1 = turn_block(1, vg1, "bank2", nc.vector.tensor_copy)
+        vg2 = gather_scalar("vg2", vpool[2], lst, after="vpool1")
+        finish(1, vt1)
         vg3 = gather_halves(vt1[:], vpool[3])
         vt2 = turn_block(2, vg2, "bank3", nc.scalar.copy, after="vpool3")
         vt3 = turn_block(3, vg3, "bank0", nc.scalar.copy)

@@ -43,10 +43,10 @@ def tile_attend_two_caches_kernel(tc, query, keys_words, keys_scales, rkey_words
         upool = [sbuf("upool%d" % k, [P, U], F32) for k in range(NB)]
         ident = sbuf("ident", [P, P], F32)
 
+        nc.gpsimd.memset(rs[:].bitcast(I32), 0)
+        nc.gpsimd.memset(ks[:].bitcast(I32), 0)
         nc.gpsimd.dma_start(out=szc[:], in_=size[0].rearrange("(p t) -> p t", t=4))
         nc.gpsimd.dma_start(out=rszc[:], in_=rsz[0].rearrange("(p t) -> p t", t=4))
-        nc.vector.memset(rs[:].bitcast(I32), 0)
-        nc.vector.memset(ks[:].bitcast(I32), 0)
         make_identity(nc, ident[:])
 
         def load_scales(plane, scales, row):
@@ -55,10 +55,10 @@ def tile_attend_two_caches_kernel(tc, query, keys_words, keys_scales, rkey_words
 
         nc.sync.dma_start(out=rw[:].bitcast(I32), in_=rkey_words[0].bitcast(I32))
         nc.sync.dma_start(lst2[:], offs2)
-        nc.sync.dma_start(lst[:], offs)
+        nc.sync.dma_start(out=qraw[:], in_=query.rearrange("(p j) w -> p j w", j=4))
         load_scales(rs, rkey_scales, 0)
         nc.sync.dma_start(out=kw[:].bitcast(I32), in_=keys_words[0].rearrange("p n t -> p (n t)").bitcast(I32))
-        nc.sync.dma_start(out=qraw[:], in_=query.rearrange("(p j) w -> p j w", j=4))
+        nc.sync.dma_start(lst[:], offs)
         load_scales(ks, keys_scales, 4)
 
         def load_rval(k):
@@ -114,10 +114,10 @@ def tile_attend_two_caches_kernel(tc, query, keys_words, keys_scales, rkey_words
 
         rwg = gather_packed("rwg", rw, lst2, U16)
         rsg = gather_packed("rsg", rs, lst2, U8)
-        kwg = gather_packed("kwg", kw, lst, U32)
         qb = sbuf("qb", [P, Q, 4], BF16)
         nc.scalar.activation(out=qb[:], in_=qraw[:].rearrange("p j w -> p w j"), func=ACT.Copy)
         qc, qs = quantise("q", qb[:].rearrange("p w j -> p (w j)"))
+        kwg = gather_packed("kwg", kw, lst, U32)
         ksg = gather_packed("ksg", ks, lst, U8)
 
         sc_b = ps.tile([P, J], F32, name="sc_b", tag="bank0")

@@ -39,14 +39,14 @@ def tile_attend_two_caches_kernel(tc, query, keys_words, keys_scales, rkey_words
         qraw = sbuf("qraw", [P, 4, Q], F32)
         szc = sbuf("szc", [P, 4], F32)
         rszc = sbuf("rszc", [P, 4], F32)
-        vpool = [sbuf("vpool%d" % k, [P, T], F32) for k in range(NB)]
-        upool = [sbuf("upool%d" % k, [P, U], F32) for k in range(NB)]
+        ufront = [sbuf("ufront%d" % b, [P, U], F32) for b in range(2)]
+        uback = sbuf("uback", [P, 2 * U], F32)
+        vfront = sbuf("vfront", [P, 2 * T], F32)
+        vback = [sbuf("vback%d" % b, [P, T], F32) for b in range(2)]
         ident = sbuf("ident", [P, P], F32)
 
         nc.gpsimd.memset(rs[:].bitcast(I32), 0)
         nc.gpsimd.memset(ks[:].bitcast(I32), 0)
-        nc.gpsimd.dma_start(out=szc[:], in_=size[0].rearrange("(p t) -> p t", t=4))
-        nc.gpsimd.dma_start(out=rszc[:], in_=rsz[0].rearrange("(p t) -> p t", t=4))
         make_identity(nc, ident[:])
 
         def load_scales(plane, scales, row):
@@ -60,26 +60,33 @@ def tile_attend_two_caches_kernel(tc, query, keys_words, keys_scales, rkey_words
         nc.sync.dma_start(out=kw[:].bitcast(I32), in_=keys_words[0].rearrange("p n t -> p (n t)").bitcast(I32))
         nc.sync.dma_start(lst[:], offs)
         load_scales(ks, keys_scales, 4)
-
-        def load_rval(k):
-            nc.sync.dma_start(out=upool[k][:], in_=rval[k * P : (k + 1) * P, :])
-
-        for k in range(NB):
-            load_rval(k)
-        for k in range(NB):
-            nc.sync.dma_start(out=vpool[k][:], in_=vals[k * P : (k + 1) * P, :])
+        for b in range(2):
+            nc.sync.dma_start(out=ufront[b][:], in_=rval[b : 2 * P : 2, :])
+        nc.sync.dma_start(out=szc[:], in_=size[0].rearrange("(p t) -> p t", t=4))
+        nc.sync.dma_start(out=rszc[:], in_=rsz[0].rearrange("(p t) -> p t", t=4))
+        nc.sync.dma_start(out=uback[:].rearrange("p (k u) -> p k u", k=2), in_=rval[2 * P : E, :].rearrange("(k p) u -> p k u", k=2))
+        nc.sync.dma_start(out=vfront[:], in_=vals[0 : 2 * P, :].rearrange("(p b) t -> p (b t)", b=2))
+        for k in range(2):
+            nc.sync.dma_start(out=vback[k][:], in_=vals[(2 + k) * P : (3 + k) * P, :])
 
         def in_order(picked):
             words = picked.bitcast(F32)
             return [words[:, u : 2 * P : 2] for u in range(2)]
 
+        def dealt(picked):
+            words = picked.bitcast(F32)
+            return [words[:, u * P : (u + 1) * P] for u in range(2)]
+
+        def blocks(tile):
+            return tile[:].bitcast(F32).rearrange("p (b r u) -> p b r u", r=P, u=2)
+
         def turn_words(sources, dst, tag, engine_copy=nc.scalar.copy):
             n = len(sources)
             bank = ps.tile([P, n, 2, P], F32, name="turned", tag=tag)
-            for b, halves in enumerate(sources):
+            for b, halves in reversed(list(enumerate(sources))):
                 for u in range(2):
                     nc.tensor.transpose(bank[:, b, u, :], halves[u], ident[:])
-            engine_copy(dst.bitcast(F32).rearrange("p (b r u) -> p b r u", b=n, u=2), bank[:].rearrange("p b u r -> p b r u"))
+            engine_copy(dst, bank[:].rearrange("p b u r -> p b r u"))
 
         def quantise(name, src, after=None):
             cols = src.shape[1] // 4
@@ -89,7 +96,7 @@ def tile_attend_two_caches_kernel(tc, query, keys_words, keys_scales, rkey_words
             return codes, plane
 
         def product(dst, left, lcol, right, rcol, start, stop):
-            lc, rc = slice(lcol, lcol + P), slice(rcol, rcol + P)
+            lc, rc = slice(lcol, lcol + P), slice(rcol, rcol + dst.shape[1])
             nc.tensor.matmul_mx(out=dst, lhsT=left[0][:, lc].bitcast(FP8X4), lhsT_scale=left[1][:, lc], rhs=right[0][:, rc].bitcast(FP8X4), rhs_scale=right[1][:, rc], start=start, stop=stop)
 
         def gather_packed(name, window, offsets, dtype):
@@ -104,8 +111,8 @@ def tile_attend_two_caches_kernel(tc, query, keys_words, keys_scales, rkey_words
 
         def gather_vector(name, window, offsets, after=None):
             picked = sbuf(name, [P, J], BF16, after)
-            nc.vector.tensor_copy(picked[:], window[:].indirect(offsets[:]))
-            return in_order(picked[:])
+            nc.vector.tensor_copy(picked[:].rearrange("p (u s e) -> p s u e", u=2, e=2), window.indirect(offsets[:]))
+            return dealt(picked[:])
 
         def gather_halves(picked, window):
             nc.vector.tensor_copy(picked[:, 0 : I // 2], window[:].indirect(lst[:, 0 : I // 32]))
@@ -127,86 +134,77 @@ def tile_attend_two_caches_kernel(tc, query, keys_words, keys_scales, rkey_words
         start = sbuf("start", [P, 1], F32, after="ks")
         negm = sbuf("negm", [P, 1], F32)
         neg = sbuf("neg", [P, I + J], F32)
-        nc.vector.tensor_scalar(out=neg[:, I : I + J], in0=sc_b[:], scalar1=-1.0, scalar2=BIG, op0=ALU.mult, op1=ALU.min, accum_out=start[:])
-        nc.vector.tensor_scalar(out=neg[:, 0:I], in0=sc_a[:], scalar1=-1.0, scalar2=start[:], op0=ALU.mult, op1=ALU.min, accum_out=negm[:])
+        nc.vector.tensor_scalar(out=neg[:, I : I + J].rearrange("q (u s e) -> q u s e", u=2, e=2), in0=sc_b[:].rearrange("q (s u e) -> q u s e", u=2, e=2), scalar1=-1.0, scalar2=BIG, op0=ALU.mult, op1=ALU.min, accum_out=start[:])
+        nc.vector.tensor_scalar(out=neg[:, 0:I].rearrange("q (u s e) -> q u s e", u=2, e=2), in0=sc_a[:].rearrange("q (s u e) -> q u s e", u=2, e=2), scalar1=-1.0, scalar2=start[:], op0=ALU.mult, op1=ALU.min, accum_out=negm[:])
 
-        ug0 = gather_scalar("ug0", upool[0], lst2)
-        ug1 = gather_scalar("ug1", upool[1], lst2)
-        prob = sbuf("prob", [P, I + J], F32, after="upool1")
+        ug0 = gather_scalar("ug0", ufront[0], lst2)
+        ug1 = gather_scalar("ug1", ufront[1], lst2)
+        prob = sbuf("prob", [P, I + J], F32, after="ufront1")
         z = sbuf("z", [P, 1], F32)
         nc.scalar.activation(out=prob[:], in_=neg[:], func=ACT.Exp, bias=negm[:], scale=-1.0, accum_out=z[:])
 
         spread = []
-        for name, col, tag in (("szb", szc, "bank2"), ("rszb", rszc, "bank3")):
-            bank = ps.tile([P, 4, P], F32, name=name, tag=tag)
+        for name, col, tag in (("szb", szc, "bank0"), ("rszb", rszc, "bank1")):
+            bank = ps.tile([P, 2, P, 2], F32, name=name, tag=tag)
             for t in range(4):
-                nc.tensor.transpose(bank[:, t, :], col[:, t : t + 1].to_broadcast([P, P]), ident[:])
+                nc.tensor.transpose(bank[:, t // 2, :, t % 2], col[:, t : t + 1].to_broadcast([P, P]), ident[:])
             spread.append(bank)
 
-        ug2 = gather_vector("ug2", upool[2], lst2, after="ks")
-        ug3 = gather_scalar("ug3", upool[3], lst2, after="neg")
+        ug3 = gather_vector("ug3", uback[:, U : 2 * U], lst2, after="ks")
+        ug2 = gather_scalar("ug2", uback, lst2, after="neg")
+        recent = sbuf("recent", [P, 16 * P], BF16, after="uback")
+        turn_words([ug0, ug3], blocks(recent)[:, 0:4:3], "bank2")
+        turn_words([ug1, ug2], blocks(recent)[:, 1:3], "bank3")
 
-        rz = sbuf("rz", [P, 1], F32, after="upool2")
+        rz = sbuf("rz", [P, 1], F32, after="ks")
         nc.vector.reciprocal(out=rz[:], in_=z[:])
         weights = []
         for n in range(2):
             weight = sbuf("weight%d" % n, [P, I], BF16)
             nc.vector.scalar_tensor_tensor(
-                out=weight[:].rearrange("q (s t) -> q s t", t=4),
-                in0=prob[:, n * I : (n + 1) * I].rearrange("q (s t) -> q s t", t=4),
+                out=weight[:],
+                in0=prob[:, n * I : (n + 1) * I],
                 scalar=rz[:],
-                in1=spread[n][:].rearrange("q t s -> q s t"),
+                in1=spread[n][:].rearrange("q u s e -> q (u s e)"),
                 op0=ALU.mult,
                 op1=ALU.mult,
             )
-            weights.append(in_order(weight[:]))
-        vg0 = gather_scalar("vg0", vpool[0], lst, after="upool3")
-        low = sbuf("low", [P, 8 * P], BF16, after="upool2")
-        turn_words([ug0, ug1], low[:], "bank0", nc.vector.tensor_copy)
-        low_q = quantise("lowq", low[:])
-        mid = sbuf("mid", [P, 16 * P], BF16)
-        turn_words([ug2, ug3], mid[:, 0 : 8 * P], "bank1", nc.vector.tensor_copy)
-        turn_words(weights, mid[:, 8 * P : 16 * P], "bank6", nc.vector.tensor_copy)
-        vg1 = gather_scalar("vg1", vpool[1], lst, after="vpool0")
-
-        def turn_block(k, vg, tag, engine_copy, after=None):
-            vt = sbuf("vt%d" % k, [P, 4 * P], BF16, after)
-            turn_words([vg], vt[:], tag, engine_copy)
-            return vt
-
-        vt0 = turn_block(0, vg0, "bank7", nc.vector.tensor_copy)
-        mid_q = quantise("midq", mid[:])
-        recent = [(low_q, 0), (low_q, P), (mid_q, 0), (mid_q, P)]
-        w_col, x_col = 2 * P, 3 * P
+            weights.append(dealt(weight[:]))
+        wx = sbuf("wx", [P, 8 * P], BF16)
+        turn_words(weights, blocks(wx), "bank6")
+        recent_q = quantise("recentq", recent[:], after="ks")
+        vg0 = gather_scalar("vg0", vfront, lst, after="negm")
+        vg1 = gather_vector("vg1", vfront[:, T : 2 * T], lst, after="ufront1")
+        wx_q = quantise("wxq", wx[:], after="vfront")
+        vt01 = sbuf("vt01", [P, 8 * P], BF16)
+        turn_words([vg0, vg1], blocks(vt01), "bank7")
+        vg2 = gather_vector("vg2", vback[0][:], lst, after="z")
+        vq01 = quantise("vq01", vt01[:], after="vback0")
+        w_col, x_col = 0, P
 
         front = ps.tile([P, 2 * P], F32, name="front", tag="bank4")
-        third = ps.tile([P, P], F32, name="third", tag="bank1")
+        third = ps.tile([P, P], F32, name="third", tag="bank2")
         last = ps.tile([P, P], F32, name="last", tag="bank5")
-        acc = [front[:, 0:P], front[:, P : 2 * P], third[:], last[:]]
-        for k in (2, 3):
-            product(acc[k], mid_q, x_col, recent[k][0], recent[k][1], True, False)
+        product(front[:], wx_q, x_col, recent_q, 0, True, False)
+        product(third[:], wx_q, x_col, recent_q, 2 * P, True, False)
+        product(last[:], wx_q, x_col, recent_q, 3 * P, True, False)
+        product(front[:], wx_q, w_col, vq01, 0, False, True)
 
-        def finish(k, turned, after=None):
-            vq = quantise("vq%d" % k, turned[:], after)
-            if k < 2:
-                product(acc[k], mid_q, x_col, recent[k][0], recent[k][1], True, False)
-            product(acc[k], mid_q, w_col, vq, 0, False, True)
+        def turn_block(name, vg, tag, after=None):
+            vt = sbuf(name, [P, 4 * P], BF16, after)
+            turn_words([vg], blocks(vt), tag)
+            return vt
 
-        def store(name, bank, col, engine_copy, queue, after=None):
-            width = bank.shape[1]
+        def store(name, sums, col, width, engine_copy, queue, after=None):
             res = sbuf(name, [P, width], F32, after)
-            engine_copy(res[:], bank[:])
+            engine_copy(res[:], sums)
             queue.dma_start(out=out[:, col : col + width], in_=res[:])
 
-        finish(0, vt0)
-        vt1 = turn_block(1, vg1, "bank2", nc.vector.tensor_copy)
-        vg2 = gather_scalar("vg2", vpool[2], lst, after="vpool1")
-        finish(1, vt1)
-        vg3 = gather_halves(vt1[:], vpool[3])
-        vt2 = turn_block(2, vg2, "bank3", nc.scalar.copy, after="vpool3")
-        vt3 = turn_block(3, vg3, "bank0", nc.scalar.copy)
-        store("res_front", front, 0, nc.vector.tensor_copy, nc.sync, after="vt1")
-        finish(2, vt2)
-        finish(3, vt3)
-        store("res_third", third, 2 * P, nc.vector.tensor_copy, nc.sync, after="vt3")
-        store("res_last", last, 3 * P, nc.scalar.copy, nc.scalar)
+        vg3 = gather_halves(recent[:, 0:I], vback[1])
+        vt2 = turn_block("vt2", vg2, "bank3", after="vback1")
+        vt3 = turn_block("vt3", vg3, "bank0")
+        store("res_front", front[:].rearrange("q (b n) -> q n b", b=2), 0, 2 * P, nc.vector.tensor_copy, nc.sync, after="uback")
+        product(third[:], wx_q, w_col, quantise("vq2", vt2[:]), 0, False, True)
+        product(last[:], wx_q, w_col, quantise("vq3", vt3[:]), 0, False, True)
+        store("res_third", third[:], 2 * P, P, nc.vector.tensor_copy, nc.sync, after="vt3")
+        store("res_last", last[:], 3 * P, P, nc.scalar.copy, nc.scalar)

@@ -190,9 +190,9 @@ def tile_attend_two_caches_kernel(tc, query, keys_words, keys_scales, rkey_words
         product(last[:], wx_q, x_col, recent_q, 3 * P, True, False)
         product(front[:], wx_q, w_col, vq01, 0, False, True)
 
-        def turn_block(name, vg, tag, after=None):
+        def turn_block(name, vg, tag, engine_copy, after=None):
             vt = sbuf(name, [P, 4 * P], BF16, after)
-            turn_words([vg], blocks(vt), tag)
+            turn_words([vg], blocks(vt), tag, engine_copy)
             return vt
 
         def store(name, sums, col, width, engine_copy, queue, after=None):
@@ -201,10 +201,10 @@ def tile_attend_two_caches_kernel(tc, query, keys_words, keys_scales, rkey_words
             queue.dma_start(out=out[:, col : col + width], in_=res[:])
 
         vg3 = gather_halves(recent[:, 0:I], vback[1])
-        vt2 = turn_block("vt2", vg2, "bank3", after="vback1")
-        vt3 = turn_block("vt3", vg3, "bank0")
-        store("res_front", front[:].rearrange("q (b n) -> q n b", b=2), 0, 2 * P, nc.vector.tensor_copy, nc.sync, after="uback")
+        vt2 = turn_block("vt2", vg2, "bank3", nc.vector.tensor_copy, after="vback1")
+        vt3 = turn_block("vt3", vg3, "bank0", nc.scalar.copy)
         product(third[:], wx_q, w_col, quantise("vq2", vt2[:]), 0, False, True)
+        store("res_front", front[:].rearrange("q (b n) -> q n b", b=2), 0, 2 * P, nc.vector.tensor_copy, nc.sync, after="vback1")
         product(last[:], wx_q, w_col, quantise("vq3", vt3[:]), 0, False, True)
         store("res_third", third[:], 2 * P, P, nc.vector.tensor_copy, nc.sync, after="vt3")
         store("res_last", last[:], 3 * P, P, nc.scalar.copy, nc.scalar)

@@ -63,8 +63,8 @@ def tile_attend_two_caches_kernel(tc, query, keys_words, keys_scales, rkey_words
         for b in range(2):
             nc.sync.dma_start(out=ufront[b][:], in_=rval[b : 2 * P : 2, :])
         nc.sync.dma_start(out=szc[:], in_=size[0].rearrange("(p t) -> p t", t=4))
-        nc.sync.dma_start(out=rszc[:], in_=rsz[0].rearrange("(p t) -> p t", t=4))
         nc.sync.dma_start(out=uback[:].rearrange("p (k u) -> p k u", k=2), in_=rval[2 * P : E, :].rearrange("(k p) u -> p k u", k=2))
+        nc.sync.dma_start(out=rszc[:], in_=rsz[0].rearrange("(p t) -> p t", t=4))
         nc.sync.dma_start(out=vfront[:], in_=vals[0 : 2 * P, :].rearrange("(p b) t -> p (b t)", b=2))
         for k in range(2):
             nc.sync.dma_start(out=vback[k][:], in_=vals[(2 + k) * P : (3 + k) * P, :])
@@ -80,10 +80,10 @@ def tile_attend_two_caches_kernel(tc, query, keys_words, keys_scales, rkey_words
         def blocks(tile):
             return tile[:].bitcast(F32).rearrange("p (b r u) -> p b r u", r=P, u=2)
 
-        def turn_words(sources, dst, tag, engine_copy=nc.scalar.copy):
+        def turn_words(sources, dst, tag, engine_copy=nc.scalar.copy, first=-1):
             n = len(sources)
             bank = ps.tile([P, n, 2, P], F32, name="turned", tag=tag)
-            for b, halves in reversed(list(enumerate(sources))):
+            for b, halves in list(enumerate(sources))[::first]:
                 for u in range(2):
                     nc.tensor.transpose(bank[:, b, u, :], halves[u], ident[:])
             engine_copy(dst, bank[:].rearrange("p b u r -> p b r u"))
@@ -152,11 +152,8 @@ def tile_attend_two_caches_kernel(tc, query, keys_words, keys_scales, rkey_words
 
         ug3 = gather_vector("ug3", uback[:, U : 2 * U], lst2, after="ks")
         ug2 = gather_scalar("ug2", uback, lst2, after="neg")
-        recent = sbuf("recent", [P, 16 * P], BF16, after="uback")
-        turn_words([ug0, ug3], blocks(recent)[:, 0:4:3], "bank2")
-        turn_words([ug1, ug2], blocks(recent)[:, 1:3], "bank3")
 
-        rz = sbuf("rz", [P, 1], F32, after="ks")
+        rz = sbuf("rz", [P, 1], F32, after="rszc")
         nc.vector.reciprocal(out=rz[:], in_=z[:])
         weights = []
         for n in range(2):
@@ -170,11 +167,14 @@ def tile_attend_two_caches_kernel(tc, query, keys_words, keys_scales, rkey_words
                 op1=ALU.mult,
             )
             weights.append(dealt(weight[:]))
-        wx = sbuf("wx", [P, 8 * P], BF16)
-        turn_words(weights, blocks(wx), "bank6")
-        recent_q = quantise("recentq", recent[:], after="ks")
+        recent = sbuf("recent", [P, 8 * P], BF16, after="ufront1")
+        turn_words([ug0, ug1], blocks(recent), "bank2", nc.vector.tensor_copy)
+        wx = sbuf("wx", [P, 16 * P], BF16)
+        turn_words([ug2, ug3], blocks(wx)[:, 2:4], "bank3", first=1)
+        turn_words(weights, blocks(wx)[:, 0:2], "bank6")
+        recent_q = quantise("recentq", recent[:])
         vg0 = gather_scalar("vg0", vfront, lst, after="negm")
-        vg1 = gather_vector("vg1", vfront[:, T : 2 * T], lst, after="ufront1")
+        vg1 = gather_vector("vg1", vfront[:, T : 2 * T], lst, after="weight0")
         wx_q = quantise("wxq", wx[:], after="vfront")
         vt01 = sbuf("vt01", [P, 8 * P], BF16)
         turn_words([vg0, vg1], blocks(vt01), "bank7")
@@ -186,8 +186,8 @@ def tile_attend_two_caches_kernel(tc, query, keys_words, keys_scales, rkey_words
         third = ps.tile([P, P], F32, name="third", tag="bank2")
         last = ps.tile([P, P], F32, name="last", tag="bank5")
         product(front[:], wx_q, x_col, recent_q, 0, True, False)
-        product(third[:], wx_q, x_col, recent_q, 2 * P, True, False)
-        product(last[:], wx_q, x_col, recent_q, 3 * P, True, False)
+        product(third[:], wx_q, x_col, wx_q, 2 * P, True, False)
+        product(last[:], wx_q, x_col, wx_q, 3 * P, True, False)
         product(front[:], wx_q, w_col, vq01, 0, False, True)
 
         def turn_block(name, vg, tag, engine_copy, after=None):

@@ -30,6 +30,8 @@ def tile_attend_two_caches_kernel(tc, query, keys_words, keys_scales, rkey_words
         def sbuf(name, shape, dtype, after=None):
             return sb.tile(shape, dtype, name=name, tag=after or name, align_bytes=64)
 
+        tail = ctx.enter_context(tc.tile_pool(name="tail", bufs=1))
+
         lst = sbuf("lst", [P, I // 16], U16)
         lst2 = sbuf("lst2", [P, J // 16], U16)
         kw = sbuf("kw", [P, T], U32)
@@ -42,7 +44,7 @@ def tile_attend_two_caches_kernel(tc, query, keys_words, keys_scales, rkey_words
         ufront = [sbuf("ufront%d" % b, [P, U], F32) for b in range(2)]
         uback = sbuf("uback", [P, 2 * U], F32)
         vfront = sbuf("vfront", [P, 2 * T], F32)
-        vback = [sbuf("vback%d" % b, [P, T], F32) for b in range(2)]
+        vback = [sbuf("vback0", [P, T], F32), tail.tile([P, T], F32, name="vback1", offset=0, align_bytes=64)]
         ident = sbuf("ident", [P, P], F32)
 
         nc.gpsimd.memset(rs[:].bitcast(I32), 0)
@@ -190,21 +192,18 @@ def tile_attend_two_caches_kernel(tc, query, keys_words, keys_scales, rkey_words
         product(last[:], wx_q, x_col, wx_q, 3 * P, True, False)
         product(front[:], wx_q, w_col, vq01, 0, False, True)
 
-        def turn_block(name, vg, tag, engine_copy, after=None):
-            vt = sbuf(name, [P, 4 * P], BF16, after)
-            turn_words([vg], blocks(vt), tag, engine_copy)
-            return vt
-
-        def store(name, sums, col, width, engine_copy, queue, after=None):
-            res = sbuf(name, [P, width], F32, after)
+        def store(res, sums, col, engine_copy, queue):
             engine_copy(res[:], sums)
-            queue.dma_start(out=out[:, col : col + width], in_=res[:])
+            queue.dma_start(out=out[:, col : col + res.shape[1]], in_=res[:])
 
         vg3 = gather_halves(recent[:, 0:I], vback[1])
-        vt2 = turn_block("vt2", vg2, "bank3", nc.vector.tensor_copy, after="vback1")
-        vt3 = turn_block("vt3", vg3, "bank0", nc.scalar.copy)
+        vt2 = tail.tile([P, 4 * P], BF16, name="vt2", offset=0, align_bytes=64)
+        turn_words([vg2], blocks(vt2), "bank3", nc.vector.tensor_copy)
+        res_front = tail.tile([P, 2 * P], F32, name="res_front", offset=1024, align_bytes=64)
+        store(res_front, front[:].rearrange("q (b n) -> q n b", b=2), 0, nc.scalar.copy, nc.sync)
+        vt3 = sbuf("vt3", [P, 4 * P], BF16)
+        turn_words([vg3], blocks(vt3), "bank0")
         product(third[:], wx_q, w_col, quantise("vq2", vt2[:]), 0, False, True)
-        store("res_front", front[:].rearrange("q (b n) -> q n b", b=2), 0, 2 * P, nc.vector.tensor_copy, nc.sync, after="vback1")
         product(last[:], wx_q, w_col, quantise("vq3", vt3[:]), 0, False, True)
-        store("res_third", third[:], 2 * P, P, nc.vector.tensor_copy, nc.sync, after="vt3")
-        store("res_last", last[:], 3 * P, P, nc.scalar.copy, nc.scalar)
+        store(sbuf("res_third", [P, P], F32, after="vt3"), third[:], 2 * P, nc.vector.tensor_copy, nc.sync)
+        store(sbuf("res_last", [P, P], F32), last[:], 3 * P, nc.scalar.copy, nc.scalar)

@@ -198,12 +198,12 @@ def tile_attend_two_caches_kernel(tc, query, keys_words, keys_scales, rkey_words
 
         vg3 = gather_halves(recent[:, 0:I], vback[1])
         vt2 = tail.tile([P, 4 * P], BF16, name="vt2", offset=0, align_bytes=64)
-        turn_words([vg2], blocks(vt2), "bank3", nc.vector.tensor_copy)
+        turn_words([vg2], blocks(vt2), "bank3")
         res_front = tail.tile([P, 2 * P], F32, name="res_front", offset=1024, align_bytes=64)
-        store(res_front, front[:].rearrange("q (b n) -> q n b", b=2), 0, nc.scalar.copy, nc.sync)
+        store(res_front, front[:].rearrange("q (b n) -> q n b", b=2), 0, nc.vector.tensor_copy, nc.sync)
         vt3 = sbuf("vt3", [P, 4 * P], BF16)
         turn_words([vg3], blocks(vt3), "bank0")
         product(third[:], wx_q, w_col, quantise("vq2", vt2[:]), 0, False, True)
         product(last[:], wx_q, w_col, quantise("vq3", vt3[:]), 0, False, True)
-        store(sbuf("res_third", [P, P], F32, after="vt3"), third[:], 2 * P, nc.vector.tensor_copy, nc.sync)
+        store(sbuf("res_third", [P, P], F32), third[:], 2 * P, nc.scalar.copy, nc.sync)
         store(sbuf("res_last", [P, P], F32), last[:], 3 * P, nc.scalar.copy, nc.scalar)

@@ -63,9 +63,9 @@ def tile_attend_two_caches_kernel(tc, query, keys_words, keys_scales, rkey_words
         nc.sync.dma_start(lst[:], offs)
         load_scales(ks, keys_scales, 4)
         for b in range(2):
-            nc.sync.dma_start(out=ufront[b][:], in_=rval[b : 2 * P : 2, :])
+            nc.sync.dma_start(out=ufront[b][:], in_=rval[(2 + b) * P : (3 + b) * P, :])
         nc.sync.dma_start(out=szc[:], in_=size[0].rearrange("(p t) -> p t", t=4))
-        nc.sync.dma_start(out=uback[:].rearrange("p (k u) -> p k u", k=2), in_=rval[2 * P : E, :].rearrange("(k p) u -> p k u", k=2))
+        nc.sync.dma_start(out=uback[:], in_=rval[0 : 2 * P, :].rearrange("(p b) u -> p (b u)", b=2))
         nc.sync.dma_start(out=rszc[:], in_=rsz[0].rearrange("(p t) -> p t", t=4))
         nc.sync.dma_start(out=vfront[:], in_=vals[0 : 2 * P, :].rearrange("(p b) t -> p (b t)", b=2))
         for k in range(2):
@@ -187,9 +187,9 @@ def tile_attend_two_caches_kernel(tc, query, keys_words, keys_scales, rkey_words
         front = ps.tile([P, 2 * P], F32, name="front", tag="bank4")
         third = ps.tile([P, P], F32, name="third", tag="bank2")
         last = ps.tile([P, P], F32, name="last", tag="bank5")
-        product(front[:], wx_q, x_col, recent_q, 0, True, False)
-        product(third[:], wx_q, x_col, wx_q, 2 * P, True, False)
-        product(last[:], wx_q, x_col, wx_q, 3 * P, True, False)
+        product(front[:], wx_q, x_col, wx_q, 2 * P, True, False)
+        product(third[:], wx_q, x_col, recent_q, 0, True, False)
+        product(last[:], wx_q, x_col, recent_q, P, True, False)
         product(front[:], wx_q, w_col, vq01, 0, False, True)
 
         def store(res, sums, col, engine_copy, queue):

@@ -45,28 +45,27 @@ def tile_attend_two_caches_kernel(tc, query, keys_words, keys_scales, rkey_words
         uback = sbuf("uback", [P, 2 * U], F32)
         vfront = sbuf("vfront", [P, 2 * T], F32)
         vback = [sbuf("vback0", [P, T], F32), tail.tile([P, T], F32, name="vback1", offset=0, align_bytes=64)]
+        planes = sbuf("planes", [P, J + I], U8)
         ident = sbuf("ident", [P, P], F32)
 
         nc.gpsimd.memset(rs[:].bitcast(I32), 0)
         nc.gpsimd.memset(ks[:].bitcast(I32), 0)
+        nc.gpsimd.memset(planes[:].bitcast(I32), 0)
         make_identity(nc, ident[:])
 
-        def load_scales(plane, scales, row):
-            for r in range(4):
-                nc.sync.dma_start(out=plane[row + r : P : 32, :].bitcast(I32), in_=scales[0, r : 16 : 4, :].bitcast(I32))
-
-        nc.sync.dma_start(out=rw[:].bitcast(I32), in_=rkey_words[0].bitcast(I32))
-        nc.sync.dma_start(lst2[:], offs2)
+        staged = slice(64, P, 4)
         nc.sync.dma_start(out=qraw[:], in_=query.rearrange("(p j) w -> p j w", j=4))
-        load_scales(rs, rkey_scales, 0)
-        nc.sync.dma_start(out=kw[:].bitcast(I32), in_=keys_words[0].rearrange("p n t -> p (n t)").bitcast(I32))
+        nc.sync.dma_start(lst2[:], offs2)
+        nc.sync.dma_start(out=rs[staged, :].bitcast(I32), in_=rkey_scales[0].bitcast(I32))
+        nc.sync.dma_start(out=ufront[0][:], in_=rval[2 * P : 3 * P, :])
         nc.sync.dma_start(lst[:], offs)
-        load_scales(ks, keys_scales, 4)
-        for b in range(2):
-            nc.sync.dma_start(out=ufront[b][:], in_=rval[(2 + b) * P : (3 + b) * P, :])
+        nc.sync.dma_start(out=ks[staged, :].bitcast(I32), in_=keys_scales[0].bitcast(I32))
+        nc.sync.dma_start(out=rw[:].bitcast(I32), in_=rkey_words[0].bitcast(I32))
         nc.sync.dma_start(out=szc[:], in_=size[0].rearrange("(p t) -> p t", t=4))
-        nc.sync.dma_start(out=uback[:], in_=rval[0 : 2 * P, :].rearrange("(p b) u -> p (b u)", b=2))
+        nc.sync.dma_start(out=kw[:].bitcast(I32), in_=keys_words[0].rearrange("p n t -> p (n t)").bitcast(I32))
         nc.sync.dma_start(out=rszc[:], in_=rsz[0].rearrange("(p t) -> p t", t=4))
+        nc.sync.dma_start(out=ufront[1][:], in_=rval[3 * P : 4 * P, :])
+        nc.sync.dma_start(out=uback[:], in_=rval[0 : 2 * P, :].rearrange("(p b) u -> p (b u)", b=2))
         nc.sync.dma_start(out=vfront[:], in_=vals[0 : 2 * P, :].rearrange("(p b) t -> p (b t)", b=2))
         for k in range(2):
             nc.sync.dma_start(out=vback[k][:], in_=vals[(2 + k) * P : (3 + k) * P, :])
@@ -101,8 +100,8 @@ def tile_attend_two_caches_kernel(tc, query, keys_words, keys_scales, rkey_words
             lc, rc = slice(lcol, lcol + P), slice(rcol, rcol + dst.shape[1])
             nc.tensor.matmul_mx(out=dst, lhsT=left[0][:, lc].bitcast(FP8X4), lhsT_scale=left[1][:, lc], rhs=right[0][:, rc].bitcast(FP8X4), rhs_scale=right[1][:, rc], start=start, stop=stop)
 
-        def gather_packed(name, window, offsets, dtype):
-            picked = sbuf(name, [P, J], dtype)
+        def gather_packed(name, window, offsets, dtype, after=None):
+            picked = sbuf(name, [P, J], dtype, after)
             nc.vector.tensor_copy(picked[:], window[:].indirect(offsets[:]))
             return picked
 
@@ -121,19 +120,30 @@ def tile_attend_two_caches_kernel(tc, query, keys_words, keys_scales, rkey_words
             nc.scalar.activation(out=picked[:, I // 2 : I], in_=window[:].indirect(lst[:, I // 32 : I // 16]), func=ACT.Copy)
             return in_order(picked)
 
-        rwg = gather_packed("rwg", rw, lst2, U16)
-        rsg = gather_packed("rsg", rs, lst2, U8)
         qb = sbuf("qb", [P, Q, 4], BF16)
         nc.scalar.activation(out=qb[:], in_=qraw[:].rearrange("p j w -> p w j"), func=ACT.Copy)
-        qc, qs = quantise("q", qb[:].rearrange("p w j -> p (w j)"))
+        rows = sbuf("rows", [P, J + I], U8)
+        nc.vector.tensor_copy(rows[:, 0:J], rs[:].indirect(lst2[:]))
+        nc.vector.tensor_copy(rows[:, J : J + I], ks[:].indirect(lst[:]))
+        for r in range(4):
+            nc.scalar.dma_start(out=planes[r:P:32, :].bitcast(I32), in_=rows[64 + 4 * r : P : 16, :].bitcast(I32))
+        qc, qs = quantise("q", qb[:].rearrange("p w j -> p (w j)"), after="ks")
+        rwg = gather_packed("rwg", rw, lst2, U16, after="rs")
         kwg = gather_packed("kwg", kw, lst, U32)
-        ksg = gather_packed("ksg", ks, lst, U8)
+
+
+        spread = []
+        for name, col, tag in (("szb", szc, "bank2"), ("rszb", rszc, "bank3")):
+            bank = ps.tile([P, 2, P, 2], F32, name=name, tag=tag)
+            for t in range(4):
+                nc.tensor.transpose(bank[:, t // 2, :, t % 2], col[:, t : t + 1].to_broadcast([P, P]), ident[:])
+            spread.append(bank)
 
         sc_b = ps.tile([P, J], F32, name="sc_b", tag="bank0")
         sc_a = ps.tile([P, I], F32, name="sc_a", tag="bank1")
-        nc.tensor.matmul_mx(out=sc_b[:], lhsT=qc[:].bitcast(FP8X4), lhsT_scale=qs[:], rhs=rwg[:].bitcast(FP4X4), rhs_scale=rsg[:], start=True, stop=True)
-        nc.tensor.matmul_mx(out=sc_a[:], lhsT=qc[:].bitcast(FP8X4), lhsT_scale=qs[:], rhs=kwg[:].bitcast(FP8X4), rhs_scale=ksg[4:P, :], start=True, stop=True)
-        start = sbuf("start", [P, 1], F32, after="ks")
+        nc.tensor.matmul_mx(out=sc_b[:], lhsT=qc[:].bitcast(FP8X4), lhsT_scale=qs[:], rhs=rwg[:].bitcast(FP4X4), rhs_scale=planes[:, 0:J], start=True, stop=True)
+        nc.tensor.matmul_mx(out=sc_a[:], lhsT=qc[:].bitcast(FP8X4), lhsT_scale=qs[:], rhs=kwg[:].bitcast(FP8X4), rhs_scale=planes[:, J : J + I], start=True, stop=True)
+        start = sbuf("start", [P, 1], F32)
         negm = sbuf("negm", [P, 1], F32)
         neg = sbuf("neg", [P, I + J], F32)
         nc.vector.tensor_scalar(out=neg[:, I : I + J].rearrange("q (u s e) -> q u s e", u=2, e=2), in0=sc_b[:].rearrange("q (s u e) -> q u s e", u=2, e=2), scalar1=-1.0, scalar2=BIG, op0=ALU.mult, op1=ALU.min, accum_out=start[:])
@@ -145,17 +155,10 @@ def tile_attend_two_caches_kernel(tc, query, keys_words, keys_scales, rkey_words
         z = sbuf("z", [P, 1], F32)
         nc.scalar.activation(out=prob[:], in_=neg[:], func=ACT.Exp, bias=negm[:], scale=-1.0, accum_out=z[:])
 
-        spread = []
-        for name, col, tag in (("szb", szc, "bank0"), ("rszb", rszc, "bank1")):
-            bank = ps.tile([P, 2, P, 2], F32, name=name, tag=tag)
-            for t in range(4):
-                nc.tensor.transpose(bank[:, t // 2, :, t % 2], col[:, t : t + 1].to_broadcast([P, P]), ident[:])
-            spread.append(bank)
-
-        ug3 = gather_vector("ug3", uback[:, U : 2 * U], lst2, after="ks")
+        ug3 = gather_vector("ug3", uback[:, U : 2 * U], lst2, after="start")
         ug2 = gather_scalar("ug2", uback, lst2, after="neg")
 
-        rz = sbuf("rz", [P, 1], F32, after="rszc")
+        rz = sbuf("rz", [P, 1], F32)
         nc.vector.reciprocal(out=rz[:], in_=z[:])
         weights = []
         for n in range(2):
@@ -170,9 +173,9 @@ def tile_attend_two_caches_kernel(tc, query, keys_words, keys_scales, rkey_words
             )
             weights.append(dealt(weight[:]))
         recent = sbuf("recent", [P, 8 * P], BF16, after="ufront1")
-        turn_words([ug0, ug1], blocks(recent), "bank2", nc.vector.tensor_copy)
+        turn_words([ug0, ug1], blocks(recent), "bank0", nc.vector.tensor_copy)
         wx = sbuf("wx", [P, 16 * P], BF16)
-        turn_words([ug2, ug3], blocks(wx)[:, 2:4], "bank3", first=1)
+        turn_words([ug2, ug3], blocks(wx)[:, 2:4], "bank1", first=1)
         turn_words(weights, blocks(wx)[:, 0:2], "bank6")
         recent_q = quantise("recentq", recent[:])
         vg0 = gather_scalar("vg0", vfront, lst, after="negm")

@@ -35,21 +35,23 @@ def tile_attend_two_caches_kernel(tc, query, keys_words, keys_scales, rkey_words
         lst = sbuf("lst", [P, I // 16], U16)
         lst2 = sbuf("lst2", [P, J // 16], U16)
         kw = sbuf("kw", [P, T], U32)
-        ks = sbuf("ks", [P, T], U8)
+        head = ctx.enter_context(tc.tile_pool(name="head", bufs=1))
+        ks = head.tile([P, T], U8, name="ks", offset=0, align_bytes=64)
         rw = sbuf("rw", [P, U], U16)
         rs = sbuf("rs", [P, U], U8)
         qraw = sbuf("qraw", [P, 4, Q], F32)
-        szc = sbuf("szc", [P, 4], F32)
-        rszc = sbuf("rszc", [P, 4], F32)
-        ufront = [sbuf("ufront%d" % b, [P, U], F32) for b in range(2)]
-        uback = sbuf("uback", [P, 2 * U], F32)
-        vfront = sbuf("vfront", [P, 2 * T], F32)
+        sizes = sbuf("sizes", [P, P], F32)
+        ufront = sbuf("ufront", [P, 2 * U], F32)
+        uback = [sbuf("uback%d" % b, [P, U], F32) for b in range(2)]
+        mid = ctx.enter_context(tc.tile_pool(name="mid", bufs=1))
+        vfront = mid.tile([P, 2 * T], F32, name="vfront", offset=0, align_bytes=64)
         vback = [sbuf("vback0", [P, T], F32), tail.tile([P, T], F32, name="vback1", offset=0, align_bytes=64)]
         planes = sbuf("planes", [P, J + I], U8)
         ident = sbuf("ident", [P, P], F32)
 
         nc.gpsimd.memset(rs[:].bitcast(I32), 0)
         nc.gpsimd.memset(ks[:].bitcast(I32), 0)
+        nc.gpsimd.memset(sizes[:], 0.0)
         nc.gpsimd.memset(planes[:].bitcast(I32), 0)
         make_identity(nc, ident[:])
 
@@ -57,18 +59,13 @@ def tile_attend_two_caches_kernel(tc, query, keys_words, keys_scales, rkey_words
         nc.sync.dma_start(out=qraw[:], in_=query.rearrange("(p j) w -> p j w", j=4))
         nc.sync.dma_start(lst2[:], offs2)
         nc.sync.dma_start(out=rs[staged, :].bitcast(I32), in_=rkey_scales[0].bitcast(I32))
-        nc.sync.dma_start(out=ufront[0][:], in_=rval[2 * P : 3 * P, :])
+        nc.sync.dma_start(out=rw[:].bitcast(I32), in_=rkey_words[0].bitcast(I32))
         nc.sync.dma_start(lst[:], offs)
         nc.sync.dma_start(out=ks[staged, :].bitcast(I32), in_=keys_scales[0].bitcast(I32))
-        nc.sync.dma_start(out=rw[:].bitcast(I32), in_=rkey_words[0].bitcast(I32))
-        nc.sync.dma_start(out=szc[:], in_=size[0].rearrange("(p t) -> p t", t=4))
+        nc.sync.dma_start(out=ufront[:], in_=rval[0 : 2 * P, :].rearrange("(p b) u -> p (b u)", b=2))
+        nc.sync.dma_start(out=sizes[0:4, :], in_=size[0].rearrange("(c n) -> c n", n=P))
+        nc.sync.dma_start(out=sizes[4:8, :], in_=rsz[0].rearrange("(c n) -> c n", n=P))
         nc.sync.dma_start(out=kw[:].bitcast(I32), in_=keys_words[0].rearrange("p n t -> p (n t)").bitcast(I32))
-        nc.sync.dma_start(out=rszc[:], in_=rsz[0].rearrange("(p t) -> p t", t=4))
-        nc.sync.dma_start(out=ufront[1][:], in_=rval[3 * P : 4 * P, :])
-        nc.sync.dma_start(out=uback[:], in_=rval[0 : 2 * P, :].rearrange("(p b) u -> p (b u)", b=2))
-        nc.sync.dma_start(out=vfront[:], in_=vals[0 : 2 * P, :].rearrange("(p b) t -> p (b t)", b=2))
-        for k in range(2):
-            nc.sync.dma_start(out=vback[k][:], in_=vals[(2 + k) * P : (3 + k) * P, :])
 
         def in_order(picked):
             words = picked.bitcast(F32)
@@ -126,17 +123,29 @@ def tile_attend_two_caches_kernel(tc, query, keys_words, keys_scales, rkey_words
         nc.vector.tensor_copy(rows[:, 0:J], rs[:].indirect(lst2[:]))
         nc.vector.tensor_copy(rows[:, J : J + I], ks[:].indirect(lst[:]))
         for r in range(4):
-            nc.scalar.dma_start(out=planes[r:P:32, :].bitcast(I32), in_=rows[64 + 4 * r : P : 16, :].bitcast(I32))
-        qc, qs = quantise("q", qb[:].rearrange("p w j -> p (w j)"), after="ks")
-        rwg = gather_packed("rwg", rw, lst2, U16, after="rs")
+            nc.sync.dma_start(out=planes[r:P:32, :].bitcast(I32), in_=rows[64 + 4 * r : P : 16, :].bitcast(I32))
+        for k in range(2):
+            nc.sync.dma_start(out=uback[k][:], in_=rval[(2 + k) * P : (3 + k) * P, :])
+        nc.sync.dma_start(out=vfront[:], in_=vals[0 : 2 * P, :].rearrange("(p b) t -> p (b t)", b=2))
+        for k in range(2):
+            nc.sync.dma_start(out=vback[k][:], in_=vals[(2 + k) * P : (3 + k) * P, :])
+        qc = head.tile([P, Q], U32, name="qc", offset=0, align_bytes=64)
+        qs = sbuf("qs", [P, Q], U8)
+        nc.vector.quantize_mx(out=qc[:].bitcast(FP8X4), scales=qs[:], in_=qb[:].rearrange("p w j -> p (w j)"))
+        rwg = head.tile([P, J], U16, name="rwg", offset=1024, align_bytes=64)
+        nc.vector.tensor_copy(rwg[:], rw[:].indirect(lst2[:]))
         kwg = gather_packed("kwg", kw, lst, U32)
 
 
+        sizes_t = ps.tile([P, P], F32, name="sizes_t", tag="bank4")
+        nc.tensor.transpose(sizes_t[:], sizes[:], ident[:])
+        cols = sbuf("cols", [P, 8], F32)
+        nc.vector.tensor_copy(cols[:], sizes_t[:, 0:8])
         spread = []
-        for name, col, tag in (("szb", szc, "bank2"), ("rszb", rszc, "bank3")):
-            bank = ps.tile([P, 2, P, 2], F32, name=name, tag=tag)
-            for t in range(4):
-                nc.tensor.transpose(bank[:, t // 2, :, t % 2], col[:, t : t + 1].to_broadcast([P, P]), ident[:])
+        for n, tag in enumerate(("bank2", "bank3")):
+            bank = ps.tile([P, 2, P, 2], F32, name="spread", tag=tag)
+            for c in range(4):
+                nc.tensor.transpose(bank[:, :, 32 * c : 32 * (c + 1), :].rearrange("q u s e -> q s u e"), cols[:, 4 * n + c : 4 * n + c + 1].to_broadcast([P, P]), ident[:])
             spread.append(bank)
 
         sc_b = ps.tile([P, J], F32, name="sc_b", tag="bank0")
@@ -149,14 +158,17 @@ def tile_attend_two_caches_kernel(tc, query, keys_words, keys_scales, rkey_words
         nc.vector.tensor_scalar(out=neg[:, I : I + J].rearrange("q (u s e) -> q u s e", u=2, e=2), in0=sc_b[:].rearrange("q (s u e) -> q u s e", u=2, e=2), scalar1=-1.0, scalar2=BIG, op0=ALU.mult, op1=ALU.min, accum_out=start[:])
         nc.vector.tensor_scalar(out=neg[:, 0:I].rearrange("q (u s e) -> q u s e", u=2, e=2), in0=sc_a[:].rearrange("q (s u e) -> q u s e", u=2, e=2), scalar1=-1.0, scalar2=start[:], op0=ALU.mult, op1=ALU.min, accum_out=negm[:])
 
-        ug0 = gather_scalar("ug0", ufront[0], lst2)
-        ug1 = gather_scalar("ug1", ufront[1], lst2)
-        prob = sbuf("prob", [P, I + J], F32, after="ufront1")
+        ug0 = gather_scalar("ug0", ufront, lst2)
+        odd = sbuf("odd", [P, J], F32)
+        nc.scalar.activation(out=odd[:], in_=ufront[:, U : 2 * U].indirect(lst2[:]), func=ACT.Copy)
+        oddb = sbuf("oddb", [P, J], BF16)
+        nc.scalar.activation(out=oddb[:].rearrange("p (u s e) -> p u s e", u=2, e=2), in_=odd[:].rearrange("p (s u e) -> p u s e", u=2, e=2), func=ACT.Copy)
+        ug1 = dealt(oddb[:])
+        ug2 = gather_scalar("ug2", uback[0], lst2)
+        prob = sbuf("prob", [P, I + J], F32, after="uback0")
         z = sbuf("z", [P, 1], F32)
         nc.scalar.activation(out=prob[:], in_=neg[:], func=ACT.Exp, bias=negm[:], scale=-1.0, accum_out=z[:])
-
-        ug3 = gather_vector("ug3", uback[:, U : 2 * U], lst2, after="start")
-        ug2 = gather_scalar("ug2", uback, lst2, after="neg")
+        ug3 = gather_vector("ug3", uback[1][:], lst2, after="start")
 
         rz = sbuf("rz", [P, 1], F32)
         nc.vector.reciprocal(out=rz[:], in_=z[:])
@@ -172,34 +184,37 @@ def tile_attend_two_caches_kernel(tc, query, keys_words, keys_scales, rkey_words
                 op1=ALU.mult,
             )
             weights.append(dealt(weight[:]))
-        recent = sbuf("recent", [P, 8 * P], BF16, after="ufront1")
-        turn_words([ug0, ug1], blocks(recent), "bank0", nc.vector.tensor_copy)
-        wx = sbuf("wx", [P, 16 * P], BF16)
-        turn_words([ug2, ug3], blocks(wx)[:, 2:4], "bank1", first=1)
-        turn_words(weights, blocks(wx)[:, 0:2], "bank6")
-        recent_q = quantise("recentq", recent[:])
-        vg0 = gather_scalar("vg0", vfront, lst, after="negm")
-        vg1 = gather_vector("vg1", vfront[:, T : 2 * T], lst, after="weight0")
-        wx_q = quantise("wxq", wx[:], after="vfront")
+        recent = sbuf("recent", [P, 16 * P], BF16, after="neg")
+        turn_words([ug0, ug1], blocks(recent)[:, 0:2], "bank0")
+        turn_words([ug2, ug3], blocks(recent)[:, 2:4], "bank1")
+        vg0 = gather_scalar("vg0", vfront, lst, after="uback1")
+        vg1 = gather_vector("vg1", vfront[:, T : 2 * T], lst, after="uback0")
+        recent_c = mid.tile([P, 4 * P], U32, name="recent_c", offset=2048, align_bytes=64)
+        recent_s = sbuf("recent_s", [P, 4 * P], U8)
+        nc.vector.quantize_mx(out=recent_c[:].bitcast(FP8X4), scales=recent_s[:], in_=recent[:])
+        recent_q = (recent_c, recent_s)
+        wx = mid.tile([P, 8 * P], BF16, name="wx", offset=0, align_bytes=64)
+        turn_words(weights, blocks(wx), "bank6")
+        wx_q = quantise("wxq", wx[:])
         vt01 = sbuf("vt01", [P, 8 * P], BF16)
-        turn_words([vg0, vg1], blocks(vt01), "bank7")
-        vg2 = gather_vector("vg2", vback[0][:], lst, after="z")
-        vq01 = quantise("vq01", vt01[:], after="vback0")
+        turn_words([vg0, vg1], blocks(vt01), "bank7", nc.vector.tensor_copy)
+        vg2 = gather_scalar("vg2", vback[0], lst, after="neg")
+        vq01 = quantise("vq01", vt01[:])
         w_col, x_col = 0, P
 
         front = ps.tile([P, 2 * P], F32, name="front", tag="bank4")
         third = ps.tile([P, P], F32, name="third", tag="bank2")
         last = ps.tile([P, P], F32, name="last", tag="bank5")
-        product(front[:], wx_q, x_col, wx_q, 2 * P, True, False)
-        product(third[:], wx_q, x_col, recent_q, 0, True, False)
-        product(last[:], wx_q, x_col, recent_q, P, True, False)
+        product(front[:], wx_q, x_col, recent_q, 0, True, False)
+        product(third[:], wx_q, x_col, recent_q, 2 * P, True, False)
+        product(last[:], wx_q, x_col, recent_q, 3 * P, True, False)
         product(front[:], wx_q, w_col, vq01, 0, False, True)
 
         def store(res, sums, col, engine_copy, queue):
             engine_copy(res[:], sums)
             queue.dma_start(out=out[:, col : col + res.shape[1]], in_=res[:])
 
-        vg3 = gather_halves(recent[:, 0:I], vback[1])
+        vg3 = gather_halves(vt01[:, 0:I], vback[1])
         vt2 = tail.tile([P, 4 * P], BF16, name="vt2", offset=0, align_bytes=64)
         turn_words([vg2], blocks(vt2), "bank3")
         res_front = tail.tile([P, 2 * P], F32, name="res_front", offset=1024, align_bytes=64)

@@ -16,7 +16,7 @@ ALU = mybir.AluOpType
 
 P = 128
 D, T, I, Q, E, U, J = 512, 2048, 512, 128, 512, 1024, 512
-NB = E // P
+RUN = 16
 BIG = 3.0e38
 FLOPS = 2 * Q * D * (I + J) + 2 * Q * E * (I + J)
 
@@ -26,26 +26,32 @@ def tile_attend_two_caches_kernel(tc, query, keys_words, keys_scales, rkey_words
     with ExitStack() as ctx:
         sb = ctx.enter_context(tc.tile_pool(name="sb", bufs=1))
         ps = ctx.enter_context(tc.psum_pool(name="ps", bufs=1))
-
-        def sbuf(name, shape, dtype, after=None):
-            return sb.tile(shape, dtype, name=name, tag=after or name, align_bytes=64)
-
+        head = ctx.enter_context(tc.tile_pool(name="head", bufs=1))
+        mid = ctx.enter_context(tc.tile_pool(name="mid", bufs=1))
+        late = ctx.enter_context(tc.tile_pool(name="late", bufs=1))
         tail = ctx.enter_context(tc.tile_pool(name="tail", bufs=1))
 
+        def sbuf(name, shape, dtype):
+            return sb.tile(shape, dtype, name=name, align_bytes=64)
+
+        def placed(pool, offset, name, shape, dtype):
+            return pool.tile(shape, dtype, name=name, offset=offset, align_bytes=64)
+
+        soft = ctx.enter_context(tc.tile_pool(name="soft", bufs=1))
+        back = ctx.enter_context(tc.tile_pool(name="back", bufs=1))
         lst = sbuf("lst", [P, I // 16], U16)
         lst2 = sbuf("lst2", [P, J // 16], U16)
         kw = sbuf("kw", [P, T], U32)
-        head = ctx.enter_context(tc.tile_pool(name="head", bufs=1))
-        ks = head.tile([P, T], U8, name="ks", offset=0, align_bytes=64)
+        ks = placed(head, 0, "ks", [P, T], U8)
         rw = sbuf("rw", [P, U], U16)
         rs = sbuf("rs", [P, U], U8)
         qraw = sbuf("qraw", [P, 4, Q], F32)
         sizes = sbuf("sizes", [P, P], F32)
         ufront = sbuf("ufront", [P, 2 * U], F32)
-        uback = [sbuf("uback%d" % b, [P, U], F32) for b in range(2)]
-        mid = ctx.enter_context(tc.tile_pool(name="mid", bufs=1))
-        vfront = mid.tile([P, 2 * T], F32, name="vfront", offset=0, align_bytes=64)
-        vback = [sbuf("vback0", [P, T], F32), tail.tile([P, T], F32, name="vback1", offset=0, align_bytes=64)]
+        uback = placed(back, 0, "uback", [P, 2 * U], F32)
+        vpair = placed(mid, 0, "vpair", [P, 2 * T], F32)
+        vthird = sbuf("vthird", [P, T], F32)
+        vlast = placed(tail, 0, "vlast", [P, T], F32)
         planes = sbuf("planes", [P, J + I], U8)
         ident = sbuf("ident", [P, P], F32)
 
@@ -55,173 +61,170 @@ def tile_attend_two_caches_kernel(tc, query, keys_words, keys_scales, rkey_words
         nc.gpsimd.memset(planes[:].bitcast(I32), 0)
         make_identity(nc, ident[:])
 
-        staged = slice(64, P, 4)
+        staged = slice(32, 96, 4)
         nc.sync.dma_start(out=qraw[:], in_=query.rearrange("(p j) w -> p j w", j=4))
         nc.sync.dma_start(lst2[:], offs2)
         nc.sync.dma_start(out=rs[staged, :].bitcast(I32), in_=rkey_scales[0].bitcast(I32))
         nc.sync.dma_start(out=rw[:].bitcast(I32), in_=rkey_words[0].bitcast(I32))
         nc.sync.dma_start(lst[:], offs)
         nc.sync.dma_start(out=ks[staged, :].bitcast(I32), in_=keys_scales[0].bitcast(I32))
-        nc.sync.dma_start(out=ufront[:], in_=rval[0 : 2 * P, :].rearrange("(p b) u -> p (b u)", b=2))
+        nc.sync.dma_start(out=kw[:].bitcast(I32), in_=keys_words[0].rearrange("p n t -> p (n t)").bitcast(I32))
         nc.sync.dma_start(out=sizes[0:4, :], in_=size[0].rearrange("(c n) -> c n", n=P))
         nc.sync.dma_start(out=sizes[4:8, :], in_=rsz[0].rearrange("(c n) -> c n", n=P))
-        nc.sync.dma_start(out=kw[:].bitcast(I32), in_=keys_words[0].rearrange("p n t -> p (n t)").bitcast(I32))
+        nc.sync.dma_start(out=ufront[:], in_=rval[0 : 2 * P, :].rearrange("(p b) u -> p (b u)", b=2))
 
-        def in_order(picked):
-            words = picked.bitcast(F32)
-            return [words[:, u : 2 * P : 2] for u in range(2)]
+        def in_runs(ap):
+            return ap.rearrange("p (u g x) -> p g u x", u=2, x=RUN)
 
-        def dealt(picked):
-            words = picked.bitcast(F32)
-            return [words[:, u * P : (u + 1) * P] for u in range(2)]
+        def gather_vector(dst, window, offsets):
+            nc.vector.tensor_copy(dst, window.indirect(offsets))
 
-        def blocks(tile):
-            return tile[:].bitcast(F32).rearrange("p (b r u) -> p b r u", r=P, u=2)
+        def gather_scalar(dst, window, offsets):
+            nc.scalar.activation(out=dst, in_=window.indirect(offsets), func=ACT.Copy)
 
-        def turn_words(sources, dst, tag, engine_copy=nc.scalar.copy, first=-1):
-            n = len(sources)
-            bank = ps.tile([P, n, 2, P], F32, name="turned", tag=tag)
-            for b, halves in list(enumerate(sources))[::first]:
+        def gather_pair(picked, pair, offsets):
+            width = pair.shape[1] // 2
+            gather_scalar(in_runs(picked[0][:]), pair[:], offsets[:])
+            gather_vector(in_runs(picked[1][:]), pair[:, width : 2 * width], offsets[:])
+            return picked
+
+        def gather_halves(picked, window):
+            gather_vector(in_runs(picked[:])[:, 0:8], window[:], lst[:, 0 : I // 32])
+            gather_scalar(in_runs(picked[:])[:, 8:16], window[:], lst[:, I // 32 : I // 16])
+            return picked
+
+        def turn(sources, tag, lead=0):
+            bank = ps.tile([P, len(sources), 2, P], F32, name="turned", tag=tag)
+            for b in sorted(range(len(sources)), key=lambda b: b != lead):
+                words = sources[b][:].bitcast(F32)
                 for u in range(2):
-                    nc.tensor.transpose(bank[:, b, u, :], halves[u], ident[:])
-            engine_copy(dst, bank[:].rearrange("p b u r -> p b r u"))
+                    nc.tensor.transpose(bank[:, b, u, :], words[:, u * P : (u + 1) * P], ident[:])
+            return bank
 
-        def quantise(name, src, after=None):
+        def copy_woven(engine_copy, dst, bank):
+            engine_copy(dst[:].bitcast(F32).rearrange("p (n b u) -> p n b u", n=P, u=2), bank[:].rearrange("p b u n -> p n b u"))
+
+        def copy_apart(engine_copy, dst, bank):
+            engine_copy(dst[:].bitcast(F32).rearrange("p (b n u) -> p b n u", n=P, u=2), bank[:].rearrange("p b u n -> p b n u"))
+
+        def quantise(name, src, codes=None):
             cols = src.shape[1] // 4
-            codes = sbuf(name + "c", [P, cols], U32, after)
+            if codes is None:
+                codes = sbuf(name + "c", [P, cols], U32)
             plane = sbuf(name + "s", [P, cols], U8)
-            nc.vector.quantize_mx(out=codes[:].bitcast(FP8X4), scales=plane[:], in_=src)
+            nc.vector.quantize_mx(out=codes[:].bitcast(FP8X4), scales=plane[:], in_=src[:])
             return codes, plane
 
         def product(dst, left, lcol, right, rcol, start, stop):
             lc, rc = slice(lcol, lcol + P), slice(rcol, rcol + dst.shape[1])
             nc.tensor.matmul_mx(out=dst, lhsT=left[0][:, lc].bitcast(FP8X4), lhsT_scale=left[1][:, lc], rhs=right[0][:, rc].bitcast(FP8X4), rhs_scale=right[1][:, rc], start=start, stop=stop)
 
-        def gather_packed(name, window, offsets, dtype, after=None):
-            picked = sbuf(name, [P, J], dtype, after)
-            nc.vector.tensor_copy(picked[:], window[:].indirect(offsets[:]))
-            return picked
-
-        def gather_scalar(name, window, offsets, after=None):
-            picked = sbuf(name, [P, J], BF16, after)
-            nc.scalar.activation(out=picked[:], in_=window[:].indirect(offsets[:]), func=ACT.Copy)
-            return in_order(picked[:])
-
-        def gather_vector(name, window, offsets, after=None):
-            picked = sbuf(name, [P, J], BF16, after)
-            nc.vector.tensor_copy(picked[:].rearrange("p (u s e) -> p s u e", u=2, e=2), window.indirect(offsets[:]))
-            return dealt(picked[:])
-
-        def gather_halves(picked, window):
-            nc.vector.tensor_copy(picked[:, 0 : I // 2], window[:].indirect(lst[:, 0 : I // 32]))
-            nc.scalar.activation(out=picked[:, I // 2 : I], in_=window[:].indirect(lst[:, I // 32 : I // 16]), func=ACT.Copy)
-            return in_order(picked)
-
-        qb = sbuf("qb", [P, Q, 4], BF16)
-        nc.scalar.activation(out=qb[:], in_=qraw[:].rearrange("p j w -> p w j"), func=ACT.Copy)
+        qb = sbuf("qb", [P, Q * 4], BF16)
+        nc.scalar.activation(out=qb[:].rearrange("p (w j) -> p w j", j=4), in_=qraw[:].rearrange("p j w -> p w j"), func=ACT.Copy)
         rows = sbuf("rows", [P, J + I], U8)
-        nc.vector.tensor_copy(rows[:, 0:J], rs[:].indirect(lst2[:]))
-        nc.vector.tensor_copy(rows[:, J : J + I], ks[:].indirect(lst[:]))
+        gather_vector(rows[:, 0:J], rs[:], lst2[:])
+        gather_vector(rows[:, J : J + I], ks[:], lst[:])
         for r in range(4):
-            nc.sync.dma_start(out=planes[r:P:32, :].bitcast(I32), in_=rows[64 + 4 * r : P : 16, :].bitcast(I32))
-        for k in range(2):
-            nc.sync.dma_start(out=uback[k][:], in_=rval[(2 + k) * P : (3 + k) * P, :])
-        nc.sync.dma_start(out=vfront[:], in_=vals[0 : 2 * P, :].rearrange("(p b) t -> p (b t)", b=2))
-        for k in range(2):
-            nc.sync.dma_start(out=vback[k][:], in_=vals[(2 + k) * P : (3 + k) * P, :])
-        qc = head.tile([P, Q], U32, name="qc", offset=0, align_bytes=64)
-        qs = sbuf("qs", [P, Q], U8)
-        nc.vector.quantize_mx(out=qc[:].bitcast(FP8X4), scales=qs[:], in_=qb[:].rearrange("p w j -> p (w j)"))
-        rwg = head.tile([P, J], U16, name="rwg", offset=1024, align_bytes=64)
-        nc.vector.tensor_copy(rwg[:], rw[:].indirect(lst2[:]))
-        kwg = gather_packed("kwg", kw, lst, U32)
-
+            nc.sync.dma_start(out=planes[r:P:32, :].bitcast(I32), in_=rows[32 + 4 * r : 96 : 16, :].bitcast(I32))
+        nc.sync.dma_start(out=uback[:], in_=rval[2 * P : 4 * P, :].rearrange("(p b) u -> p (b u)", b=2))
+        nc.sync.dma_start(out=vpair[:], in_=vals[0 : 2 * P, :].rearrange("(p b) t -> p (b t)", b=2))
+        nc.sync.dma_start(out=vthird[:], in_=vals[2 * P : 3 * P, :])
+        nc.sync.dma_start(out=vlast[:], in_=vals[3 * P : 4 * P, :])
+        qc, qs = quantise("q", qb, placed(head, 0, "qc", [P, Q], U32))
+        rwg = placed(head, 1024, "rwg", [P, J], U16)
+        gather_vector(rwg[:], rw[:], lst2[:])
+        kwg = sbuf("kwg", [P, I], U32)
+        gather_vector(kwg[:], kw[:], lst[:])
 
         sizes_t = ps.tile([P, P], F32, name="sizes_t", tag="bank4")
         nc.tensor.transpose(sizes_t[:], sizes[:], ident[:])
         cols = sbuf("cols", [P, 8], F32)
-        nc.vector.tensor_copy(cols[:], sizes_t[:, 0:8])
+        nc.scalar.copy(cols[:], sizes_t[:, 0:8])
         spread = []
         for n, tag in enumerate(("bank2", "bank3")):
-            bank = ps.tile([P, 2, P, 2], F32, name="spread", tag=tag)
+            bank = ps.tile([P, I], F32, name="spread", tag=tag)
             for c in range(4):
-                nc.tensor.transpose(bank[:, :, 32 * c : 32 * (c + 1), :].rearrange("q u s e -> q s u e"), cols[:, 4 * n + c : 4 * n + c + 1].to_broadcast([P, P]), ident[:])
+                nc.tensor.transpose(in_runs(bank[:])[:, 4 * c : 4 * (c + 1)], cols[:, 4 * n + c : 4 * n + c + 1].to_broadcast([P, P]), ident[:])
             spread.append(bank)
+
+        unrounded = sbuf("unrounded", [P, J], F32)
+        gather_scalar(unrounded[:], ufront[:, U : 2 * U], lst2[:])
+        ug0 = sbuf("ug0", [P, J], BF16)
+        gather_scalar(in_runs(ug0[:]), ufront[:], lst2[:])
 
         sc_b = ps.tile([P, J], F32, name="sc_b", tag="bank0")
         sc_a = ps.tile([P, I], F32, name="sc_a", tag="bank1")
         nc.tensor.matmul_mx(out=sc_b[:], lhsT=qc[:].bitcast(FP8X4), lhsT_scale=qs[:], rhs=rwg[:].bitcast(FP4X4), rhs_scale=planes[:, 0:J], start=True, stop=True)
         nc.tensor.matmul_mx(out=sc_a[:], lhsT=qc[:].bitcast(FP8X4), lhsT_scale=qs[:], rhs=kwg[:].bitcast(FP8X4), rhs_scale=planes[:, J : J + I], start=True, stop=True)
-        start = sbuf("start", [P, 1], F32)
+        start = placed(late, 0, "start", [P, 1], F32)
         negm = sbuf("negm", [P, 1], F32)
-        neg = sbuf("neg", [P, I + J], F32)
-        nc.vector.tensor_scalar(out=neg[:, I : I + J].rearrange("q (u s e) -> q u s e", u=2, e=2), in0=sc_b[:].rearrange("q (s u e) -> q u s e", u=2, e=2), scalar1=-1.0, scalar2=BIG, op0=ALU.mult, op1=ALU.min, accum_out=start[:])
-        nc.vector.tensor_scalar(out=neg[:, 0:I].rearrange("q (u s e) -> q u s e", u=2, e=2), in0=sc_a[:].rearrange("q (s u e) -> q u s e", u=2, e=2), scalar1=-1.0, scalar2=start[:], op0=ALU.mult, op1=ALU.min, accum_out=negm[:])
+        neg = placed(late, 2048, "neg", [P, I + J], F32)
 
-        ug0 = gather_scalar("ug0", ufront, lst2)
-        odd = sbuf("odd", [P, J], F32)
-        nc.scalar.activation(out=odd[:], in_=ufront[:, U : 2 * U].indirect(lst2[:]), func=ACT.Copy)
-        oddb = sbuf("oddb", [P, J], BF16)
-        nc.scalar.activation(out=oddb[:].rearrange("p (u s e) -> p u s e", u=2, e=2), in_=odd[:].rearrange("p (s u e) -> p u s e", u=2, e=2), func=ACT.Copy)
-        ug1 = dealt(oddb[:])
-        ug2 = gather_scalar("ug2", uback[0], lst2)
-        prob = sbuf("prob", [P, I + J], F32, after="uback0")
+        def by_halves(ap):
+            return ap.rearrange("q (g u x) -> q u g x", u=2, x=RUN)
+
+        def by_blocks(ap):
+            return ap.rearrange("p (g u x) -> p g u x", u=2, x=RUN)
+
+        def as_laid(ap):
+            return ap.rearrange("q (u g x) -> q u g x", u=2, x=RUN)
+
+        nc.vector.tensor_scalar(out=as_laid(neg[:, I : I + J]), in0=by_halves(sc_b[:]), scalar1=-1.0, scalar2=BIG, op0=ALU.mult, op1=ALU.min, accum_out=start[:])
+        ug1 = placed(head, 1024, "ug1", [P, J], BF16)
+        nc.vector.tensor_copy(in_runs(ug1[:]), by_blocks(unrounded[:]))
+        nc.vector.tensor_scalar(out=as_laid(neg[:, 0:I]), in0=by_halves(sc_a[:]), scalar1=-1.0, scalar2=start[:], op0=ALU.mult, op1=ALU.min, accum_out=negm[:])
+        ug23 = [placed(late, 4096, "ug2", [P, J], BF16), placed(late, 0, "ug3", [P, J], BF16)]
+        gather_vector(in_runs(ug23[1][:]), uback[:, U : 2 * U], lst2[:])
+        prob = placed(soft, 0, "prob", [P, I + J], F32)
         z = sbuf("z", [P, 1], F32)
         nc.scalar.activation(out=prob[:], in_=neg[:], func=ACT.Exp, bias=negm[:], scale=-1.0, accum_out=z[:])
-        ug3 = gather_vector("ug3", uback[1][:], lst2, after="start")
-
         rz = sbuf("rz", [P, 1], F32)
         nc.vector.reciprocal(out=rz[:], in_=z[:])
         weights = []
         for n in range(2):
             weight = sbuf("weight%d" % n, [P, I], BF16)
-            nc.vector.scalar_tensor_tensor(
-                out=weight[:],
-                in0=prob[:, n * I : (n + 1) * I],
-                scalar=rz[:],
-                in1=spread[n][:].rearrange("q u s e -> q (u s e)"),
-                op0=ALU.mult,
-                op1=ALU.mult,
-            )
-            weights.append(dealt(weight[:]))
-        recent = sbuf("recent", [P, 16 * P], BF16, after="neg")
-        turn_words([ug0, ug1], blocks(recent)[:, 0:2], "bank0")
-        turn_words([ug2, ug3], blocks(recent)[:, 2:4], "bank1")
-        vg0 = gather_scalar("vg0", vfront, lst, after="uback1")
-        vg1 = gather_vector("vg1", vfront[:, T : 2 * T], lst, after="uback0")
-        recent_c = mid.tile([P, 4 * P], U32, name="recent_c", offset=2048, align_bytes=64)
-        recent_s = sbuf("recent_s", [P, 4 * P], U8)
-        nc.vector.quantize_mx(out=recent_c[:].bitcast(FP8X4), scales=recent_s[:], in_=recent[:])
-        recent_q = (recent_c, recent_s)
-        wx = mid.tile([P, 8 * P], BF16, name="wx", offset=0, align_bytes=64)
-        turn_words(weights, blocks(wx), "bank6")
-        wx_q = quantise("wxq", wx[:])
-        vt01 = sbuf("vt01", [P, 8 * P], BF16)
-        turn_words([vg0, vg1], blocks(vt01), "bank7", nc.vector.tensor_copy)
-        vg2 = gather_scalar("vg2", vback[0], lst, after="neg")
-        vq01 = quantise("vq01", vt01[:])
+            nc.vector.scalar_tensor_tensor(out=weight[:], in0=prob[:, n * I : (n + 1) * I], scalar=rz[:], in1=spread[n][:], op0=ALU.mult, op1=ALU.mult)
+            weights.append(weight)
+
+        gather_scalar(in_runs(ug23[0][:]), uback[:], lst2[:])
+        ut01 = placed(late, 2048, "ut01", [P, 8 * P], BF16)
+        copy_woven(nc.scalar.copy, ut01, turn([ug0, ug1], "bank5", lead=1))
+        ut23 = sbuf("ut23", [P, 8 * P], BF16)
+        copy_woven(nc.scalar.copy, ut23, turn(ug23, "bank0", lead=1))
+        uq01 = quantise("uq01", ut01, placed(soft, 0, "uq01c", [P, 2 * P], U32))
+        weights_t = turn(weights, "bank6")
+
+        vg01 = gather_pair([sbuf("vg0", [P, I], BF16), sbuf("vg1", [P, I], BF16)], vpair, lst)
+        wx = placed(mid, 0, "wx", [P, 8 * P], BF16)
+        copy_apart(nc.scalar.copy, wx, weights_t)
+        uq23 = quantise("uq23", ut23, placed(mid, 2048, "uq23c", [P, 2 * P], U32))
+        wq = quantise("wq", wx)
+        vt01 = placed(soft, 4096, "vt01", [P, 8 * P], BF16)
+        copy_woven(nc.vector.tensor_copy, vt01, turn(vg01, "bank7"))
+        vg2 = placed(mid, 4096, "vg2", [P, I], BF16)
+        gather_scalar(in_runs(vg2[:]), vthird[:], lst[:])
+        vq01 = quantise("vq01", vt01)
         w_col, x_col = 0, P
 
         front = ps.tile([P, 2 * P], F32, name="front", tag="bank4")
-        third = ps.tile([P, P], F32, name="third", tag="bank2")
-        last = ps.tile([P, P], F32, name="last", tag="bank5")
-        product(front[:], wx_q, x_col, recent_q, 0, True, False)
-        product(third[:], wx_q, x_col, recent_q, 2 * P, True, False)
-        product(last[:], wx_q, x_col, recent_q, 3 * P, True, False)
-        product(front[:], wx_q, w_col, vq01, 0, False, True)
+        third = ps.tile([P, P], F32, name="third", tag="bank5")
+        last = ps.tile([P, P], F32, name="last", tag="bank3")
+        product(front[:], wq, x_col, uq01, 0, True, False)
+        product(third[:], wq, x_col, uq23, 0, True, False)
+        product(last[:], wq, x_col, uq23, P, True, False)
+        product(front[:], wq, w_col, vq01, 0, False, True)
 
         def store(res, sums, col, engine_copy, queue):
-            engine_copy(res[:], sums)
+            engine_copy(res[:], sums[:])
             queue.dma_start(out=out[:, col : col + res.shape[1]], in_=res[:])
 
-        vg3 = gather_halves(vt01[:, 0:I], vback[1])
-        vt2 = tail.tile([P, 4 * P], BF16, name="vt2", offset=0, align_bytes=64)
-        turn_words([vg2], blocks(vt2), "bank3")
-        res_front = tail.tile([P, 2 * P], F32, name="res_front", offset=1024, align_bytes=64)
-        store(res_front, front[:].rearrange("q (b n) -> q n b", b=2), 0, nc.vector.tensor_copy, nc.sync)
+        vg3 = gather_halves(placed(soft, 4096, "vg3", [P, I], BF16), vlast)
+        vt2 = placed(tail, 0, "vt2", [P, 4 * P], BF16)
+        copy_apart(nc.scalar.copy, vt2, turn([vg2], "bank2"))
+        store(placed(tail, 1024, "res_front", [P, 2 * P], F32), front, 0, nc.vector.tensor_copy, nc.sync)
         vt3 = sbuf("vt3", [P, 4 * P], BF16)
-        turn_words([vg3], blocks(vt3), "bank0")
-        product(third[:], wx_q, w_col, quantise("vq2", vt2[:]), 0, False, True)
-        product(last[:], wx_q, w_col, quantise("vq3", vt3[:]), 0, False, True)
-        store(sbuf("res_third", [P, P], F32), third[:], 2 * P, nc.scalar.copy, nc.sync)
-        store(sbuf("res_last", [P, P], F32), last[:], 3 * P, nc.scalar.copy, nc.scalar)
+        copy_apart(nc.scalar.copy, vt3, turn([vg3], "bank1"))
+        product(third[:], wq, w_col, quantise("vq2", vt2), 0, False, True)
+        product(last[:], wq, w_col, quantise("vq3", vt3), 0, False, True)
+        store(sbuf("res_third", [P, P], F32), third, 2 * P, nc.scalar.copy, nc.sync)
+        store(sbuf("res_last", [P, P], F32), last, 3 * P, nc.scalar.copy, nc.scalar)

@@ -58,8 +58,8 @@ def tile_attend_two_caches_kernel(tc, query, keys_words, keys_scales, rkey_words
         nc.gpsimd.memset(rs[:].bitcast(I32), 0)
         nc.gpsimd.memset(ks[:].bitcast(I32), 0)
         nc.gpsimd.memset(sizes[:], 0.0)
-        nc.gpsimd.memset(planes[:].bitcast(I32), 0)
         make_identity(nc, ident[:])
+        nc.gpsimd.memset(planes[:].bitcast(I32), 0)
 
         staged = slice(32, 96, 4)
         nc.sync.dma_start(out=qraw[:], in_=query.rearrange("(p j) w -> p j w", j=4))
@@ -222,9 +222,14 @@ def tile_attend_two_caches_kernel(tc, query, keys_words, keys_scales, rkey_words
         vt2 = placed(tail, 0, "vt2", [P, 4 * P], BF16)
         copy_apart(nc.scalar.copy, vt2, turn([vg2], "bank2"))
         store(placed(tail, 1024, "res_front", [P, 2 * P], F32), front, 0, nc.vector.tensor_copy, nc.sync)
-        vt3 = sbuf("vt3", [P, 4 * P], BF16)
-        copy_apart(nc.scalar.copy, vt3, turn([vg3], "bank1"))
+        last_t = turn([vg3], "bank1")
+        vt3 = [sbuf("vt3_%d" % h, [P, 2 * P], BF16) for h in range(2)]
+        for h in range(2):
+            nc.scalar.copy(vt3[h][:].bitcast(F32).rearrange("p (n u) -> p n u", u=2), last_t[:, 0, :, h * 64 : (h + 1) * 64].rearrange("p u n -> p n u"))
         product(third[:], wq, w_col, quantise("vq2", vt2), 0, False, True)
-        product(last[:], wq, w_col, quantise("vq3", vt3), 0, False, True)
+        vq3 = (sbuf("vq3c", [P, P], U32), sbuf("vq3s", [P, P], U8))
+        for h in range(2):
+            nc.vector.quantize_mx(out=vq3[0][:, h * 64 : (h + 1) * 64].bitcast(FP8X4), scales=vq3[1][:, h * 64 : (h + 1) * 64], in_=vt3[h][:])
+        product(last[:], wq, w_col, vq3, 0, False, True)
         store(sbuf("res_third", [P, P], F32), third, 2 * P, nc.scalar.copy, nc.sync)
-        store(sbuf("res_last", [P, P], F32), last, 3 * P, nc.scalar.copy, nc.scalar)
+        store(sbuf("res_last", [P, P], F32), last, 3 * P, nc.vector.tensor_copy, nc.scalar)

@@ -218,7 +218,7 @@ def tile_attend_two_caches_kernel(tc, query, keys_words, keys_scales, rkey_words
             engine_copy(res[:], sums[:])
             queue.dma_start(out=out[:, col : col + res.shape[1]], in_=res[:])
 
-        vg3 = gather_halves(placed(soft, 4096, "vg3", [P, I], BF16), vlast)
+        vg3 = gather_halves(sbuf("vg3", [P, I], BF16), vlast)
         vt2 = placed(tail, 0, "vt2", [P, 4 * P], BF16)
         copy_apart(nc.scalar.copy, vt2, turn([vg2], "bank2"))
         store(placed(tail, 1024, "res_front", [P, 2 * P], F32), front, 0, nc.vector.tensor_copy, nc.sync)

@@ -231,5 +231,5 @@ def tile_attend_two_caches_kernel(tc, query, keys_words, keys_scales, rkey_words
         for h in range(2):
             nc.vector.quantize_mx(out=vq3[0][:, h * 64 : (h + 1) * 64].bitcast(FP8X4), scales=vq3[1][:, h * 64 : (h + 1) * 64], in_=vt3[h][:])
         product(last[:], wq, w_col, vq3, 0, False, True)
-        store(sbuf("res_third", [P, P], F32), third, 2 * P, nc.scalar.copy, nc.sync)
+        store(sbuf("res_third", [P, P], F32), third, 2 * P, nc.scalar.copy, nc.scalar)
         store(sbuf("res_last", [P, P], F32), last, 3 * P, nc.vector.tensor_copy, nc.scalar)

@@ -50,7 +50,7 @@ def tile_attend_two_caches_kernel(tc, query, keys_words, keys_scales, rkey_words
         ufront = sbuf("ufront", [P, 2 * U], F32)
         uback = placed(back, 0, "uback", [P, 2 * U], F32)
         vpair = placed(mid, 0, "vpair", [P, 2 * T], F32)
-        vthird = sbuf("vthird", [P, T], F32)
+        vthird = placed(back, 8192, "vthird", [P, T], F32)
         vlast = placed(tail, 0, "vlast", [P, T], F32)
         planes = sbuf("planes", [P, J + I], U8)
         ident = sbuf("ident", [P, P], F32)
@@ -105,7 +105,7 @@ def tile_attend_two_caches_kernel(tc, query, keys_words, keys_scales, rkey_words
             engine_copy(dst[:].bitcast(F32).rearrange("p (n b u) -> p n b u", n=P, u=2), bank[:].rearrange("p b u n -> p n b u"))
 
         def copy_apart(engine_copy, dst, bank):
-            engine_copy(dst[:].bitcast(F32).rearrange("p (b n u) -> p b n u", n=P, u=2), bank[:].rearrange("p b u n -> p b n u"))
+            engine_copy(dst[:].bitcast(F32).rearrange("p (b n u) -> p b n u", n=P, u=2), bank.rearrange("p b u n -> p b n u"))
 
         def quantise(name, src, codes=None):
             cols = src.shape[1] // 4
@@ -115,9 +115,9 @@ def tile_attend_two_caches_kernel(tc, query, keys_words, keys_scales, rkey_words
             nc.vector.quantize_mx(out=codes[:].bitcast(FP8X4), scales=plane[:], in_=src[:])
             return codes, plane
 
-        def product(dst, left, lcol, right, rcol, start, stop):
-            lc, rc = slice(lcol, lcol + P), slice(rcol, rcol + dst.shape[1])
-            nc.tensor.matmul_mx(out=dst, lhsT=left[0][:, lc].bitcast(FP8X4), lhsT_scale=left[1][:, lc], rhs=right[0][:, rc].bitcast(FP8X4), rhs_scale=right[1][:, rc], start=start, stop=stop)
+        def product(dst, left, right, rcol, start, stop):
+            rc = slice(rcol, rcol + dst.shape[1])
+            nc.tensor.matmul_mx(out=dst, lhsT=left[0][:].bitcast(FP8X4), lhsT_scale=left[1][:], rhs=right[0][:, rc].bitcast(FP8X4), rhs_scale=right[1][:, rc], start=start, stop=stop)
 
         qb = sbuf("qb", [P, Q * 4], BF16)
         nc.scalar.activation(out=qb[:].rearrange("p (w j) -> p w j", j=4), in_=qraw[:].rearrange("p j w -> p w j"), func=ACT.Copy)
@@ -195,24 +195,26 @@ def tile_attend_two_caches_kernel(tc, query, keys_words, keys_scales, rkey_words
         weights_t = turn(weights, "bank6")
 
         vg01 = gather_pair([sbuf("vg0", [P, I], BF16), sbuf("vg1", [P, I], BF16)], vpair, lst)
-        wx = placed(mid, 0, "wx", [P, 8 * P], BF16)
-        copy_apart(nc.scalar.copy, wx, weights_t)
+        xt = placed(mid, 0, "xt", [P, 4 * P], BF16)
+        copy_apart(nc.scalar.copy, xt, weights_t[:, 1:2])
+        wt = placed(mid, 1024, "wt", [P, 4 * P], BF16)
+        copy_apart(nc.scalar.copy, wt, weights_t[:, 0:1])
         uq23 = quantise("uq23", ut23, placed(mid, 2048, "uq23c", [P, 2 * P], U32))
-        wq = quantise("wq", wx)
+        xq = quantise("xq", xt)
+        wq = quantise("wq", wt)
         vt01 = placed(soft, 4096, "vt01", [P, 8 * P], BF16)
         copy_woven(nc.vector.tensor_copy, vt01, turn(vg01, "bank7"))
         vg2 = placed(mid, 4096, "vg2", [P, I], BF16)
         gather_scalar(in_runs(vg2[:]), vthird[:], lst[:])
-        vq01 = quantise("vq01", vt01)
-        w_col, x_col = 0, P
+        vq01 = quantise("vq01", vt01, placed(back, 8192, "vq01c", [P, 2 * P], U32))
 
         front = ps.tile([P, 2 * P], F32, name="front", tag="bank4")
         third = ps.tile([P, P], F32, name="third", tag="bank5")
         last = ps.tile([P, P], F32, name="last", tag="bank3")
-        product(front[:], wq, x_col, uq01, 0, True, False)
-        product(third[:], wq, x_col, uq23, 0, True, False)
-        product(last[:], wq, x_col, uq23, P, True, False)
-        product(front[:], wq, w_col, vq01, 0, False, True)
+        product(front[:], xq, uq01, 0, True, False)
+        product(third[:], xq, uq23, 0, True, False)
+        product(last[:], xq, uq23, P, True, False)
+        product(front[:], wq, vq01, 0, False, True)
 
         def store(res, sums, col, engine_copy, queue):
             engine_copy(res[:], sums[:])
@@ -220,16 +222,16 @@ def tile_attend_two_caches_kernel(tc, query, keys_words, keys_scales, rkey_words
 
         vg3 = gather_halves(sbuf("vg3", [P, I], BF16), vlast)
         vt2 = placed(tail, 0, "vt2", [P, 4 * P], BF16)
-        copy_apart(nc.scalar.copy, vt2, turn([vg2], "bank2"))
+        copy_apart(nc.scalar.copy, vt2, turn([vg2], "bank2")[:])
         store(placed(tail, 1024, "res_front", [P, 2 * P], F32), front, 0, nc.vector.tensor_copy, nc.sync)
         last_t = turn([vg3], "bank1")
         vt3 = [sbuf("vt3_%d" % h, [P, 2 * P], BF16) for h in range(2)]
         for h in range(2):
             nc.scalar.copy(vt3[h][:].bitcast(F32).rearrange("p (n u) -> p n u", u=2), last_t[:, 0, :, h * 64 : (h + 1) * 64].rearrange("p u n -> p n u"))
-        product(third[:], wq, w_col, quantise("vq2", vt2), 0, False, True)
+        product(third[:], wq, quantise("vq2", vt2), 0, False, True)
         vq3 = (sbuf("vq3c", [P, P], U32), sbuf("vq3s", [P, P], U8))
         for h in range(2):
             nc.vector.quantize_mx(out=vq3[0][:, h * 64 : (h + 1) * 64].bitcast(FP8X4), scales=vq3[1][:, h * 64 : (h + 1) * 64], in_=vt3[h][:])
-        product(last[:], wq, w_col, vq3, 0, False, True)
+        product(last[:], wq, vq3, 0, False, True)
         store(sbuf("res_third", [P, P], F32), third, 2 * P, nc.scalar.copy, nc.scalar)
         store(sbuf("res_last", [P, P], F32), last, 3 * P, nc.vector.tensor_copy, nc.scalar)

from contextlib import ExitStack

import concourse.mybir as mybir
from concourse.masks import make_identity

F32 = mybir.dt.float32
BF16 = mybir.dt.bfloat16
I32 = mybir.dt.int32
U32 = mybir.dt.uint32
U16 = mybir.dt.uint16
U8 = mybir.dt.uint8
FP8X4 = mybir.dt.float8_e4m3fn_x4
FP4X4 = mybir.dt.float4_e2m1fn_x4
ACT = mybir.ActivationFunctionType
ALU = mybir.AluOpType

P = 128
D, T, I, Q, E, U, J = 512, 2048, 512, 128, 512, 1024, 512
RUN = 16
BIG = 3.0e38
FLOPS = 2 * Q * D * (I + J) + 2 * Q * E * (I + J)


def tile_attend_two_caches_kernel(tc, query, keys_words, keys_scales, rkey_words, rkey_scales, size, rsz, vals, rval, offs, offs2, out):
    nc = tc.nc
    with ExitStack() as ctx:
        sb = ctx.enter_context(tc.tile_pool(name="sb", bufs=1))
        ps = ctx.enter_context(tc.psum_pool(name="ps", bufs=1))
        head = ctx.enter_context(tc.tile_pool(name="head", bufs=1))
        mid = ctx.enter_context(tc.tile_pool(name="mid", bufs=1))
        late = ctx.enter_context(tc.tile_pool(name="late", bufs=1))
        tail = ctx.enter_context(tc.tile_pool(name="tail", bufs=1))

        def sbuf(name, shape, dtype):
            return sb.tile(shape, dtype, name=name, align_bytes=64)

        def placed(pool, offset, name, shape, dtype):
            return pool.tile(shape, dtype, name=name, offset=offset, align_bytes=64)

        soft = ctx.enter_context(tc.tile_pool(name="soft", bufs=1))
        back = ctx.enter_context(tc.tile_pool(name="back", bufs=1))
        lst = sbuf("lst", [P, I // 16], U16)
        lst2 = sbuf("lst2", [P, J // 16], U16)
        kw = sbuf("kw", [P, T], U32)
        ks = placed(head, 0, "ks", [P, T], U8)
        rw = sbuf("rw", [P, U], U16)
        rs = sbuf("rs", [P, U], U8)
        qraw = sbuf("qraw", [P, 4, Q], F32)
        sizes = sbuf("sizes", [P, P], F32)
        ufront = sbuf("ufront", [P, 2 * U], F32)
        uback = placed(back, 0, "uback", [P, 2 * U], F32)
        vpair = placed(mid, 0, "vpair", [P, 2 * T], F32)
        vthird = placed(back, 8192, "vthird", [P, T], F32)
        vlast = placed(tail, 0, "vlast", [P, T], F32)
        planes = sbuf("planes", [P, J + I], U8)
        ident = sbuf("ident", [P, P], F32)

        nc.gpsimd.memset(rs[:].bitcast(I32), 0)
        nc.gpsimd.memset(ks[:].bitcast(I32), 0)
        nc.gpsimd.memset(sizes[:], 0.0)
        make_identity(nc, ident[:])
        nc.gpsimd.memset(planes[:].bitcast(I32), 0)

        staged = slice(32, 96, 4)
        nc.sync.dma_start(out=qraw[:], in_=query.rearrange("(p j) w -> p j w", j=4))
        nc.sync.dma_start(lst2[:], offs2)
        nc.sync.dma_start(out=rs[staged, :].bitcast(I32), in_=rkey_scales[0].bitcast(I32))
        nc.sync.dma_start(out=rw[:].bitcast(I32), in_=rkey_words[0].bitcast(I32))
        nc.sync.dma_start(lst[:], offs)
        nc.sync.dma_start(out=ks[staged, :].bitcast(I32), in_=keys_scales[0].bitcast(I32))
        nc.sync.dma_start(out=kw[:].bitcast(I32), in_=keys_words[0].rearrange("p n t -> p (n t)").bitcast(I32))
        nc.sync.dma_start(out=sizes[0:4, :], in_=size[0].rearrange("(c n) -> c n", n=P))
        nc.sync.dma_start(out=sizes[4:8, :], in_=rsz[0].rearrange("(c n) -> c n", n=P))
        nc.sync.dma_start(out=ufront[:], in_=rval[0 : 2 * P, :].rearrange("(p b) u -> p (b u)", b=2))

        def in_runs(ap):
            return ap.rearrange("p (u g x) -> p g u x", u=2, x=RUN)

        def gather_vector(dst, window, offsets):
            nc.vector.tensor_copy(dst, window.indirect(offsets))

        def gather_scalar(dst, window, offsets):
            nc.scalar.activation(out=dst, in_=window.indirect(offsets), func=ACT.Copy)

        def gather_pair(picked, pair, offsets):
            width = pair.shape[1] // 2
            gather_scalar(in_runs(picked[0][:]), pair[:], offsets[:])
            gather_vector(in_runs(picked[1][:]), pair[:, width : 2 * width], offsets[:])
            return picked

        def gather_halves(picked, window):
            gather_vector(in_runs(picked[:])[:, 0:8], window[:], lst[:, 0 : I // 32])
            gather_scalar(in_runs(picked[:])[:, 8:16], window[:], lst[:, I // 32 : I // 16])
            return picked

        def turn(sources, tag, lead=0):
            bank = ps.tile([P, len(sources), 2, P], F32, name="turned", tag=tag)
            for b in sorted(range(len(sources)), key=lambda b: b != lead):
                words = sources[b][:].bitcast(F32)
                for u in range(2):
                    nc.tensor.transpose(bank[:, b, u, :], words[:, u * P : (u + 1) * P], ident[:])
            return bank

        def copy_woven(engine_copy, dst, bank):
            engine_copy(dst[:].bitcast(F32).rearrange("p (n b u) -> p n b u", n=P, u=2), bank[:].rearrange("p b u n -> p n b u"))

        def copy_apart(engine_copy, dst, bank):
            engine_copy(dst[:].bitcast(F32).rearrange("p (b n u) -> p b n u", n=P, u=2), bank.rearrange("p b u n -> p b n u"))

        def quantise(name, src, codes=None):
            cols = src.shape[1] // 4
            if codes is None:
                codes = sbuf(name + "c", [P, cols], U32)
            plane = sbuf(name + "s", [P, cols], U8)
            nc.vector.quantize_mx(out=codes[:].bitcast(FP8X4), scales=plane[:], in_=src[:])
            return codes, plane

        def product(dst, left, right, rcol, start, stop):
            rc = slice(rcol, rcol + dst.shape[1])
            nc.tensor.matmul_mx(out=dst, lhsT=left[0][:].bitcast(FP8X4), lhsT_scale=left[1][:], rhs=right[0][:, rc].bitcast(FP8X4), rhs_scale=right[1][:, rc], start=start, stop=stop)

        qb = sbuf("qb", [P, Q * 4], BF16)
        nc.scalar.activation(out=qb[:].rearrange("p (w j) -> p w j", j=4), in_=qraw[:].rearrange("p j w -> p w j"), func=ACT.Copy)
        rows = sbuf("rows", [P, J + I], U8)
        gather_vector(rows[:, 0:J], rs[:], lst2[:])
        gather_vector(rows[:, J : J + I], ks[:], lst[:])
        for r in range(4):
            nc.sync.dma_start(out=planes[r:P:32, :].bitcast(I32), in_=rows[32 + 4 * r : 96 : 16, :].bitcast(I32))
        nc.sync.dma_start(out=uback[:], in_=rval[2 * P : 4 * P, :].rearrange("(p b) u -> p (b u)", b=2))
        nc.sync.dma_start(out=vpair[:], in_=vals[0 : 2 * P, :].rearrange("(p b) t -> p (b t)", b=2))
        nc.sync.dma_start(out=vthird[:], in_=vals[2 * P : 3 * P, :])
        nc.sync.dma_start(out=vlast[:], in_=vals[3 * P : 4 * P, :])
        qc, qs = quantise("q", qb, placed(head, 0, "qc", [P, Q], U32))
        rwg = placed(head, 1024, "rwg", [P, J], U16)
        gather_vector(rwg[:], rw[:], lst2[:])
        kwg = sbuf("kwg", [P, I], U32)
        gather_vector(kwg[:], kw[:], lst[:])

        sizes_t = ps.tile([P, P], F32, name="sizes_t", tag="bank4")
        nc.tensor.transpose(sizes_t[:], sizes[:], ident[:])
        cols = sbuf("cols", [P, 8], F32)
        nc.scalar.copy(cols[:], sizes_t[:, 0:8])
        spread = []
        for n, tag in enumerate(("bank2", "bank3")):
            bank = ps.tile([P, I], F32, name="spread", tag=tag)
            for c in range(4):
                nc.tensor.transpose(in_runs(bank[:])[:, 4 * c : 4 * (c + 1)], cols[:, 4 * n + c : 4 * n + c + 1].to_broadcast([P, P]), ident[:])
            spread.append(bank)

        unrounded = sbuf("unrounded", [P, J], F32)
        gather_scalar(unrounded[:], ufront[:, U : 2 * U], lst2[:])
        ug0 = sbuf("ug0", [P, J], BF16)
        gather_scalar(in_runs(ug0[:]), ufront[:], lst2[:])

        sc_b = ps.tile([P, J], F32, name="sc_b", tag="bank0")
        sc_a = ps.tile([P, I], F32, name="sc_a", tag="bank1")
        nc.tensor.matmul_mx(out=sc_b[:], lhsT=qc[:].bitcast(FP8X4), lhsT_scale=qs[:], rhs=rwg[:].bitcast(FP4X4), rhs_scale=planes[:, 0:J], start=True, stop=True)
        nc.tensor.matmul_mx(out=sc_a[:], lhsT=qc[:].bitcast(FP8X4), lhsT_scale=qs[:], rhs=kwg[:].bitcast(FP8X4), rhs_scale=planes[:, J : J + I], start=True, stop=True)
        start = placed(late, 0, "start", [P, 1], F32)
        negm = sbuf("negm", [P, 1], F32)
        neg = placed(late, 2048, "neg", [P, I + J], F32)

        def by_halves(ap):
            return ap.rearrange("q (g u x) -> q u g x", u=2, x=RUN)

        def by_blocks(ap):
            return ap.rearrange("p (g u x) -> p g u x", u=2, x=RUN)

        def as_laid(ap):
            return ap.rearrange("q (u g x) -> q u g x", u=2, x=RUN)

        nc.vector.tensor_scalar(out=as_laid(neg[:, I : I + J]), in0=by_halves(sc_b[:]), scalar1=-1.0, scalar2=BIG, op0=ALU.mult, op1=ALU.min, accum_out=start[:])
        ug1 = placed(head, 1024, "ug1", [P, J], BF16)
        nc.vector.tensor_copy(in_runs(ug1[:]), by_blocks(unrounded[:]))
        nc.vector.tensor_scalar(out=as_laid(neg[:, 0:I]), in0=by_halves(sc_a[:]), scalar1=-1.0, scalar2=start[:], op0=ALU.mult, op1=ALU.min, accum_out=negm[:])
        ug23 = [placed(late, 4096, "ug2", [P, J], BF16), placed(late, 0, "ug3", [P, J], BF16)]
        gather_vector(in_runs(ug23[1][:]), uback[:, U : 2 * U], lst2[:])
        prob = placed(soft, 0, "prob", [P, I + J], F32)
        z = sbuf("z", [P, 1], F32)
        nc.scalar.activation(out=prob[:], in_=neg[:], func=ACT.Exp, bias=negm[:], scale=-1.0, accum_out=z[:])
        rz = sbuf("rz", [P, 1], F32)
        nc.vector.reciprocal(out=rz[:], in_=z[:])
        weights = []
        for n in range(2):
            weight = sbuf("weight%d" % n, [P, I], BF16)
            nc.vector.scalar_tensor_tensor(out=weight[:], in0=prob[:, n * I : (n + 1) * I], scalar=rz[:], in1=spread[n][:], op0=ALU.mult, op1=ALU.mult)
            weights.append(weight)

        gather_scalar(in_runs(ug23[0][:]), uback[:], lst2[:])
        ut01 = placed(late, 2048, "ut01", [P, 8 * P], BF16)
        copy_woven(nc.scalar.copy, ut01, turn([ug0, ug1], "bank5", lead=1))
        ut23 = sbuf("ut23", [P, 8 * P], BF16)
        copy_woven(nc.scalar.copy, ut23, turn(ug23, "bank0", lead=1))
        uq01 = quantise("uq01", ut01, placed(soft, 0, "uq01c", [P, 2 * P], U32))
        weights_t = turn(weights, "bank6")

        vg01 = gather_pair([sbuf("vg0", [P, I], BF16), sbuf("vg1", [P, I], BF16)], vpair, lst)
        xt = placed(mid, 0, "xt", [P, 4 * P], BF16)
        copy_apart(nc.scalar.copy, xt, weights_t[:, 1:2])
        wt = placed(mid, 1024, "wt", [P, 4 * P], BF16)
        copy_apart(nc.scalar.copy, wt, weights_t[:, 0:1])
        uq23 = quantise("uq23", ut23, placed(mid, 2048, "uq23c", [P, 2 * P], U32))
        xq = quantise("xq", xt)
        wq = quantise("wq", wt)
        vt01 = placed(soft, 4096, "vt01", [P, 8 * P], BF16)
        copy_woven(nc.vector.tensor_copy, vt01, turn(vg01, "bank7"))
        vg2 = placed(mid, 4096, "vg2", [P, I], BF16)
        gather_scalar(in_runs(vg2[:]), vthird[:], lst[:])
        vq01 = quantise("vq01", vt01, placed(back, 8192, "vq01c", [P, 2 * P], U32))

        front = ps.tile([P, 2 * P], F32, name="front", tag="bank4")
        third = ps.tile([P, P], F32, name="third", tag="bank5")
        last = ps.tile([P, P], F32, name="last", tag="bank3")
        product(front[:], xq, uq01, 0, True, False)
        product(third[:], xq, uq23, 0, True, False)
        product(last[:], xq, uq23, P, True, False)
        product(front[:], wq, vq01, 0, False, True)

        def store(res, sums, col, engine_copy, queue):
            engine_copy(res[:], sums[:])
            queue.dma_start(out=out[:, col : col + res.shape[1]], in_=res[:])

        vg3 = gather_halves(sbuf("vg3", [P, I], BF16), vlast)
        vt2 = placed(tail, 0, "vt2", [P, 4 * P], BF16)
        copy_apart(nc.scalar.copy, vt2, turn([vg2], "bank2")[:])
        store(placed(tail, 1024, "res_front", [P, 2 * P], F32), front, 0, nc.vector.tensor_copy, nc.sync)
        last_t = turn([vg3], "bank1")
        vt3 = [sbuf("vt3_%d" % h, [P, 2 * P], BF16) for h in range(2)]
        for h in range(2):
            nc.scalar.copy(vt3[h][:].bitcast(F32).rearrange("p (n u) -> p n u", u=2), last_t[:, 0, :, h * 64 : (h + 1) * 64].rearrange("p u n -> p n u"))
        product(third[:], wq, quantise("vq2", vt2), 0, False, True)
        vq3 = (sbuf("vq3c", [P, P], U32), sbuf("vq3s", [P, P], U8))
        for h in range(2):
            nc.vector.quantize_mx(out=vq3[0][:, h * 64 : (h + 1) * 64].bitcast(FP8X4), scales=vq3[1][:, h * 64 : (h + 1) * 64], in_=vt3[h][:])
        product(last[:], wq, vq3, 0, False, True)
        store(sbuf("res_third", [P, P], F32), third, 2 * P, nc.scalar.copy, nc.scalar)
        store(sbuf("res_last", [P, P], F32), last, 3 * P, nc.vector.tensor_copy, nc.scalar)
